import numpy as np, ml_dtypes
CORES = [3,11,19,27,35,43,51,59]
N = 8
BF = ml_dtypes.bfloat16
def f(rng, *shape):
    return (rng.standard_normal(shape, dtype=np.float32) * np.exp2(rng.integers(-2, 3, shape[:-1] + (1,)))).astype(BF)
def wide(rng, *shape):
    v = f(rng, *shape).astype(np.float32); k = shape[:-2] + (1, shape[-1])
    return (v * np.exp2(rng.integers(-6, 7, k)) * (rng.random(k) > 0.0625)).astype(BF)
M, K, TR, CAP = 2048, 64, 4, 192
D = 16 * K
def hashes(s, n):
    lo = ((s & 4095) + 1597 * n) & 4095; b = ((s >> 12) + ((lo * lo) >> 6)) & 4095
    return (lo + ((b * b) >> 6)) & 4095, b
def seed_of(a, b, n):
    lo = (a - ((b * b) >> 6)) & 4095
    return ((b - ((lo * lo) >> 6)) & 4095) * 4096 + ((lo - 1597 * n) & 4095)
def owners(t, s):
    a, b = hashes(np.asarray(s, np.int64)[..., None], (TR + 1) * np.arange(K)); w = (a * N) >> 12
    return np.where(b < t[w], w, t[N + w]).astype(np.int64)
def loads(t, s):
    o = owners(t, s); return np.stack([np.sum(o == q, -1) for q in range(N)], -1)
def sixteen(rng, t, keep=()):
    m = 16 - len(keep); kept = np.array(keep, np.int64); base = np.sum(loads(t, kept), 0)
    pool = rng.integers(0, 1 << 24, 1024); c = loads(t, pool); ok = np.flatnonzero(np.all(c * m <= CAP - base, 1)); j = np.arange(m)
    for u in range(m):
        if np.all(np.sum(c[j], 0) + base <= CAP): break
        j[u] = rng.choice(ok)
    return rng.permutation(np.concatenate([pool[j], kept]))
def ranks(rng, least):
    return np.concatenate([rng.integers(least, 4097, N), rng.permutation(N)]).astype(np.int64)
def absent(rng):
    w = rng.permutation(N); t = np.zeros(2 * N, np.int64)
    t[w] = (8192 * np.arange(N) + N - 1) // (2 * (N - 1)); t[N + w] = np.roll(w, -1); return t
def history(rng, dens):
    w = np.zeros((N, 128, M), np.float32)
    for q in range(N):
        for r in range(N):
            w[q] += np.float32(2 ** r) * (rng.random((128, M), dtype=np.float32) < dens[r][:, None])
    return w.astype(BF)
def seeds(rng, rk):
    return np.stack([np.stack([sixteen(rng, rk[g]) for g in range(8)]) for r in range(N)])
def complete(rng, rk, sd, dens=None):
    if dens is None: dens = rng.choice(np.array([0.1, 0.5, 0.9]), (N, 128))
    return {"sd": np.reshape(sd, (N, 128, 1)).astype(np.int32), "rk": np.stack([rk] * N).astype(np.int32), "thr": rng.integers(0, 4097, (N, 8, M)).astype(np.int32),
            "ali": rng.integers(0, M, (N, 8, M)).astype(np.int32), "seen": history(rng, dens), "vec": f(rng, N, 128, M)}
def setup_inputs(rng):
    rk = np.stack([ranks(rng, 2800) for g in range(8)]); return complete(rng, rk, seeds(rng, rk))
def setup_inputs_full(rng):
    o0 = rng.integers(0, N); rk = []
    for g in range(8):
        o = (o0 + g) % N; t = np.concatenate([rng.integers(3874 - 40, 3874 + 41, N), np.full(N, o)]).astype(np.int64); t[o] = 4096; rk.append(t)
    rk = np.stack(rk); sd = seeds(rng, rk); C = CAP // 16
    far = rng.integers(0, N, 8); h = rng.permutation(8); far[h[0]] = 0; far[h[1]] = rng.integers(1, N)
    for g in range(8):
        o = (o0 + g) % N; r = (o + far[g]) % N
        pool = rng.integers(0, 1 << 24, 4096); c = loads(rk[g], pool); fine = np.all(np.delete(c, o, 1) <= C, 1); s = []
        for i in range(8):
            x = rng.integers(-2, 3)
            for v in (C + x, C - x): s.append(pool[rng.choice(np.flatnonzero(fine & (c[:, o] == v)))])
        sd[r, g] = rng.permutation(np.array(s))
    return complete(rng, rk, sd)
def setup_inputs_edges(rng):
    rk, tie = [], []
    for g in range(8):
        t = ranks(rng, 3500); w = rng.permutation(N)[:4]; t[w[0]] = 0; t[N + w[0]] = w[1]; t[w[1]] = 0; t[N + w[1]] = w[0]; t[w[2]] = rng.integers(3500, 4096); t[N + w[2]] = w[0]; t[w[3]] = 4096; rk.append(t)
        tie.append(seed_of(int(w[2]) * (4096 // N) + int(rng.integers(0, 4096 // N)), int(t[w[2]]), (TR + 1) * int(rng.integers(0, K))))
    rk = np.stack(rk); sd = np.stack([np.stack([sixteen(rng, rk[g], (0, (1 << 24) - 1, tie[g])) for g in range(8)]) for r in range(N)])
    d = complete(rng, rk, sd); z = rng.integers(0, 4, (N, 8, M)); thr = np.where(z == 0, 0, np.where(z == 1, 4096, d["thr"])); z = rng.integers(0, 4, (N, 8, M))
    ali = np.where(z == 0, 0, np.where(z == 1, M - 1, np.where(z == 2, np.arange(M), d["ali"])))
    for r in range(N):
        for g in range(8):
            q = owners(rk[g], sd[r, g])[:, ::4]; a, b = hashes(sd[r, g][:, None], ((TR + 1) * np.arange(K) + 1)[None, ::4]); e = (a * M) >> 12
            thr[q, g, e] = b; ali[q, g, e] = M - 1 - e
    d["thr"] = thr.astype(np.int32); d["ali"] = ali.astype(np.int32); return d
def setup_inputs_hot(rng):
    rk = np.stack([ranks(rng, 2800) for g in range(8)]); sd = seeds(rng, rk)
    for g in range(8):
        pool = rng.integers(0, 1 << 24, 1024); sd[rng.integers(0, N), g] = pool[rng.choice(np.flatnonzero(np.all(loads(rk[g], pool) <= CAP // 16, 1)))]
    d = complete(rng, rk, sd); h = rng.integers(0, M, (N, 8, 1)); h[:, 0] = 0; h[:, 7] = M - 1
    d["thr"] = rng.integers(0, 512, (N, 8, M)).astype(np.int32); d["ali"] = (h + np.zeros((1, 1, M), np.int64)).astype(np.int32); return d
def setup_inputs_avid(rng):
    rk = np.stack([absent(rng) for g in range(8)]); dens = rng.choice(np.array([0, 0.97, 1.0]), (N, 128)); dens[rng.integers(0, N)] = 1
    return complete(rng, rk, seeds(rng, rk), dens)
def setup_inputs_spread(rng):
    d = setup_inputs(rng); d["vec"] = wide(rng, N, 128, M); d["thr"] = (4096 >> rng.integers(0, 14, (N, 8, M))).astype(np.int32); return d
def check_inputs(d):
    bad = []
    try:
        sd, rk = d["sd"].astype(np.int64), d["rk"].astype(np.int64); w = d["seen"].astype(np.float32)
        if not ((sd >= 0) & (sd < 1 << 24)).all(): bad.append("seed")
        if not (rk == rk[:1]).all(): bad.append("rk alike on all ranks")
        if not ((rk[..., :N] >= 0) & (rk[..., :N] <= 4096) & (rk[..., N:] >= 0) & (rk[..., N:] < N)).all(): bad.append("rk")
        if not ((d["thr"] >= 0) & (d["thr"] <= 4096)).all(): bad.append("thr")
        if not ((d["ali"] >= 0) & (d["ali"] < M)).all(): bad.append("ali")
        if not ((w >= 0) & (w < 2 ** N) & (w == np.floor(w))).all(): bad.append("seen")
        if not np.isfinite(d["vec"].astype(np.float32)).all(): bad.append("finite")
        if not bad and any((np.sum(loads(rk[r, g], sd[r, 16 * g:16 * g + 16, 0]), 0) > CAP).any() for r in range(N) for g in range(8)): bad.append("cap")
    except Exception:
        bad.append("unreadable")
    return bad
def reference(sd, rk, thr, ali, seen, vec):
    chosen = np.zeros((N, 128, K), np.float32); y = np.zeros((N, 128, D), vec.dtype); n = (TR + 1) * np.arange(K); row = np.arange(16)[:, None]
    for r in range(N):
        for g in range(8):
            s = sd[r, 16 * g:16 * g + 16].astype(np.int64)
            q = owners(rk[r, g].astype(np.int64), s[:, 0])
            x = np.zeros((16, K), np.int64); done = np.zeros((16, K), bool)
            for i in range(1, TR + 1):
                a, b = hashes(s, n + i); e = (a * M) >> 12
                c = np.where(b < thr[q, g, e], e, ali[q, g, e]).astype(np.int64)
                known = (seen[q, 16 * g + row, c].astype(np.float32).astype(np.int64) >> r) & 1
                x = np.where(done, x, c); done = done | (known == 0)
            chosen[r, 16 * g:16 * g + 16] = q * M + x
            y[r, 16 * g:16 * g + 16] = vec[q.T.reshape(-1), 16 * g + row, x.T.reshape(-1)]
    return {"chosen": chosen, "y": y}

@@ -1,0 +1,476 @@
+from concourse.bass import DstId, RemoteDMATransfer
+from concourse.mybir import AluOpType, ActivationFunctionType
+
+A = AluOpType
+F = ActivationFunctionType
+N = 8
+CAPQ, LC = 192, 12
+S0 = N - 1
+HS = [(0, 2), (2, 4), (4, 8)]
+CH = [(0, 2), (2, 4), (4, 6), (6, 7), (7, 8)]
+GRP = [(0, 1), (2, 3), (4, 5), (6,)]
+PLAN = [[(0, "T")],
+        [(0, "H", 0), (7, "H", 1), (24, "G", 0), (24, "A", 0), (25, "G", 1), (20, "H", 2), (22, "M", 0, 4), (34, "A", 1), (34, "G", 2)],
+        [(0, "F", 0), (0, "M", 4, 8), (1, "G", 3), (9, "A", 2), (8, "F", 1), (13, "P", 0), (17, "A", 3), (20, "G", 4), (16, "F", 2), (21, "P", 1), (25, "A", 4),
+         (24, "F", 3), (27, "P", 2), (34, "I", 0), (30, "F", 4), (33, "P", 3), (40, "I", 1), (40, "P", 4), (39, "Y"), (52, "I", 4), (53, "I", 2), (54, "I", 3)]]
+TB = ["b0", "b1", "b7"]
+f32, b16, i32, u16, f16 = "float32", "bfloat16", "int32", "uint16", "float16"
+SHAPES = {
+    i32: {"sdI": 1, "rkI": 16, "thrI": 128, "aliI": 128, "iotaK": 64,
+          "loI": 1, "hiI": 1, "Lr": 64, "Lq": 64, "t1": 64, "Bq": 64, "Lp": 64, "t2": 64, "w12": 64,
+          "F2i": 64, "ya": 64, "yb": 64, "yc": 64, "yd": 64, "own176": 64,
+          "hx": (8, 48), "hL": (8, 48), "h4": (8, 48), "hq": (8, 48), "ht": (8, 48), "hB": (8, 48), "hb": (8, 48), "hu": (8, 48), "he": (8, 48),
+          "mn": (8, 48), "cI": (8, 48), "sI": 288, "sb": (8, 36), "ky": (8, 48), "m2": (8, 24), "kc": 96, "xI": 96},
+    f32: {"rkF": 16, "onef": 128, "Rm": 128, "w1c": 8, "w4c": 8, "loF": 1, "hiF": 1, "hpF": 1, "Zk": 64, "tA": 8, "dA": 8, "dB": 8,
+          "VxS": 1024, "Vwin": 1536, "vl": (8, 12), "own2k": 64, "ot": 8, "T0": 128, "T1": 128, "T2": 128, "r1": 128,
+          "rnS": (8, 2), "rn": (8, 2), "msg": (8, 48), "rq": (8, 48), "chS": 64},
+    b16: {"seenS": 2048, "vecS": 2048, "W1": 2048, "oneb": 144, "Id": 144, "Id192": 128, "Tri": 128, "rst": 512, "Ci": 108,
+          "Zs": 144, "Za": 144, "Zb": 144, "Zt": 144, "Zi": 144, "jc": 192, "stp": 1024, "Pc": 512, "Dc": 512, "Of": 512, "ownb": 64,
+          "p0": 128, "p1": 128, "p2": 128, "p4": 128, "rs": 1536, "land": 1536, "ab": 1536, "mk": 1536, "GT": 6144, "MG": 4608,
+          "IDx": 1536, "IDg": 1024, "yS": 1024},
+    u16: {"F2u": 64, "yo": 64, "le": 384, "rl": 384, "lx": 96, "lr": 96, "ls": 288},
+    f16: {"I1": 144, "I4": 144, "Lh": 64, "Hh": 64},
+}
+SCRATCH = {}
+for _dt, _d in SHAPES.items():
+    for _k, _n in _d.items():
+        SCRATCH[_k] = ("sbuf", [128] + (list(_n) if isinstance(_n, tuple) else [_n]), _dt)
+for _b in range(8):
+    SCRATCH["b%d" % _b] = ("psum", [128, 512], f32)
+SEMAPHORES = ["sv", "ss", "st", "sg", "lsem"] + ["d%d" % _k for _k in range(32)] + ["%s%d" % (_m, _k) for _m in ("rn", "rl", "rq", "lr", "la") for _k in range(N)]
+
+
+def rank_program(g, core, T, topo):
+    me = T.rank_of(core)
+    if me is None:
+        return
+    queue = {"v": g.vector, "s": g.scalar, "t": g.tensor, "g": g, "y": g.sync}
+    count = {}
+    clock = {q: {} for q in queue}
+    seen_by = {}
+    log = {}
+    ndma = [0]
+
+    def V2(name, a=0, b=None, step=1, p=None, key=None):
+        b = SCRATCH[name][1][1] if b is None else b
+        ap = T[name][:, a:b:step] if p is None else T[name][p, a:b:step]
+        return (ap, [(key or name, a, b)])
+
+    def V3(name, s0, s1, a, b):
+        w = SCRATCH[name][1][2]
+        ap = T[name][:, s0, a:b] if s1 == s0 + 1 else T[name][:, s0:s1, a:b]
+        return (ap, [(name, s * w + a, s * w + b) for s in range(s0, s1)])
+
+    def IX(win, off):
+        return (win[0].indirect(off[0]), win[1] + off[1])
+
+    BANKS = ["b%d" % k for k in range(8)]
+
+    def need(q, reads, writes):
+        toks = []
+        for regs, w in ((reads, False), (writes, True)):
+            for (k, lo, hi) in regs:
+                for (l2, h2, w2, tok, e2) in log.get(k, []):
+                    if k in BANKS and e2 != q:
+                        toks.append(tok)
+                    elif l2 < hi and lo < h2 and (w or w2) and not (q == "t" and e2 == "t"):
+                        toks.append(tok)
+        best = {}
+        for (s, n) in toks:
+            if clock[q].get(s, 0) < n:
+                best[s] = max(best.get(s, 0), n)
+        for s in sorted(best, key=lambda s: (s[0] != "d", s)):
+            n = best[s]
+            if clock[q].get(s, 0) < n:
+                queue[q].wait_ge(T.sem[s], n)
+                clock[q][s] = n
+                for s2, n2 in seen_by.get((s, n), {}).items():
+                    clock[q][s2] = max(clock[q].get(s2, 0), n2)
+
+    def done(q, inst, reads, writes, sem, inc):
+        inst.then_inc(T.sem[sem], inc)
+        count[sem] = count.get(sem, 0) + inc
+        tok = (sem, count[sem])
+        c = dict(clock[q])
+        c[sem] = count[sem]
+        seen_by[tok] = c
+        for regs, w in ((reads, False), (writes, True)):
+            for (k, lo, hi) in regs:
+                log.setdefault(k, []).append((lo, hi, w, tok, q))
+
+    stream = [None]
+
+    def later(q, f):
+        if stream[0] is None:
+            f()
+        else:
+            stream[0].append((q, f))
+
+    def now(q, f, outs, ins):
+        reads = [r for x in ins for r in x[1]]
+        writes = [r for x in outs for r in x[1]]
+        need(q, reads, writes)
+        done(q, f(), reads, writes, "s" + q, 1)
+
+    def op(q, f, outs, ins):
+        later(q, lambda: now(q, f, outs, ins))
+
+    def isv(x):
+        return isinstance(x, tuple)
+
+    def raw(x):
+        return x[0] if isv(x) else x
+
+    def ts(out, in0, s1, s2, o0, o1=None):
+        ins = [x for x in (in0, s1, s2) if isv(x)]
+        if o1 is None:
+            op("v", lambda: g.vector.tensor_scalar(out[0], in0[0], raw(s1), None, o0), [out], ins)
+        else:
+            op("v", lambda: g.vector.tensor_scalar(out[0], in0[0], raw(s1), raw(s2), o0, o1), [out], ins)
+
+    def tt(out, a, b, o):
+        op("v", lambda: g.vector.tensor_tensor(out[0], a[0], b[0], o), [out], [a, b])
+
+    def cp(out, a):
+        op("v", lambda: g.vector.tensor_copy(out[0], a[0]), [out], [a])
+
+    def fill(out, c):
+        op("v", lambda: g.vector.memset(out[0], c), [out], [])
+
+    def act(out, a, func=F.Copy, **kw):
+        ins = [a] + [x for x in kw.values() if isv(x)]
+        k2 = {k: raw(x) for k, x in kw.items()}
+        op("s", lambda: g.scalar.activation(out[0], a[0], func, **k2), [out], ins)
+
+    def mm(out, lhs, rhs, start, stop):
+        op("t", lambda: g.tensor.matmul(out[0], lhs[0], rhs[0], start, stop), [out], [lhs, rhs])
+
+    def aff(out, a, pat, cmp, base, cm):
+        op("g", lambda: g.affine_select(out[0], a[0], pat, cmp, 0.0, base, cm), [out], [a])
+
+    def iota(out, pat, base, cm, small=False):
+        if small:
+            op("g", lambda: g.iota(out[0], pat, base, cm, allow_small_or_imprecise_dtypes=True), [out], [])
+        else:
+            op("g", lambda: g.iota(out[0], pat, base, cm), [out], [])
+
+    def dma_now(q, out, a, after):
+        need(q, a[1], out[1] + after)
+        sem = "d%d" % ndma[0]
+        ndma[0] += 1
+        done(q, queue[q].dma_start(out[0], a[0]), a[1], out[1], sem, 16)
+
+    def dma(q, out, a, after=()):
+        later(q, lambda: dma_now(q, out, a, list(after)))
+
+    def hbm(ap):
+        return (ap, [])
+
+    def send_now(pairs, sem):
+        need("g", [r for x in pairs for r in x[2][1]], [])
+        tr = []
+        for j, (s, q, a, o) in enumerate(pairs):
+            eng = topo.engines(core, T.cores[q])
+            n = len(eng) // len(pairs)
+            rid, pid, se = topo.addr(T.cores[q])
+            count["lsem"] = count.get("lsem", 0) + n
+            if len(pairs) == 1:
+                g.remote_dma(o, a[0], T.sem["%s%d" % (sem, s)], T.sem.lsem, pid, rid, topo.mask(core, T.cores[q]))
+                return
+            tr.append(RemoteDMATransfer(dst_ids=[DstId(rid=rid, pnc=pid)], dma_engine_mask=sum(1 << e for e in eng[n * j:n * j + n]),
+                                        remote_sem=T.sem["%s%d" % (sem, s)], src=a[0], dst=o))
+        g.remote_dma_fused(tr, local_sem=T.sem.lsem)
+
+    def send(pairs, sem):
+        later("g", lambda: send_now(pairs, sem))
+
+    def hops(d):
+        a, b = topo.chip(T.cores[0]), topo.chip(T.cores[d])
+        return 3 if d == 0 else 2 if topo.mates(a, b) else 1 if topo.same_plane(a, b) else 0
+
+    DIST = sorted(range(N), key=hops)
+    owner = [me ^ d for d in DIST]
+    asker = owner
+    FAR = [s for s in range(N) if s != S0]
+
+    def arrives(sem, s, src, view, together):
+        n = len(topo.engines(T.cores[src], core)) // together
+        name = "%s%d" % (sem, s)
+        count[name] = n
+        seen_by[(name, n)] = {name: n}
+        for (k, lo, hi) in view[1]:
+            log.setdefault(k, []).append((lo, hi, True, (name, n), "remote"))
+
+    for s in FAR:
+        k = [len(gr) for gr in GRP if s in gr][0]
+        arrives("rn", s, asker[s], V3("rn", s, s + 1, 0, 2), N - 1)
+        arrives("rl", s, asker[s], V2("rl", 48 * s, 48 * s + 48), k)
+        arrives("rq", s, asker[s], V3("rq", s, s + 1, 0, 48), k)
+        arrives("lr", s, owner[s], V2("lr", LC * s, LC * s + LC), k)
+        arrives("la", s, owner[s], V2("land", CAPQ * owner[s], CAPQ * owner[s] + CAPQ), k)
+
+    dma("y", V2("sdI"), hbm(T.sd[:]))
+    dma("s", V2("rkI", p=slice(0, 8)), hbm(T.rk[:]))
+    dma("y", V2("thrI"), hbm(T.thr[:]))
+    dma("s", V2("aliI"), hbm(T.ali[:]))
+    dma("y", V2("seenS"), hbm(T.seen[:]))
+    dma("y", V2("vecS"), hbm(T.vec[:]))
+
+    fill(V2("oneb"), 1.0)
+    fill(V2("onef"), 1.0)
+    fill(V2("rst"), 1.0)
+    fill(V2("rst", 0, 512, 64), 0.0)
+    fill(V2("Zs"), 0.0)
+    fill(V2("Zs", 15, 144, 16), 1.0)
+    iota(V2("iotaK"), [[7985, 64]], 0, 0)
+    iota(V2("w1c"), [[1, 8]], 0, 0, True)
+    iota(V2("w4c"), [[4096, 8]], 0, 0, True)
+    P8 = slice(0, 8)
+    aff(V2("Id"), V2("oneb"), [[-1, 144]], A.is_equal, 0, 1)
+    aff(V2("Rm", p=P8), V2("onef", 0, 128, p=P8), [[1, 128]], A.is_ge, 0, -16)
+    aff(V2("Rm", p=P8), V2("Rm", p=P8), [[-1, 128]], A.is_ge, 15, 16)
+    aff(V2("Tri"), V2("oneb", 0, 128), [[16, 8], [1, 16]], A.is_gt, 0, -1)
+    aff(V2("Tri"), V2("Tri"), [[-16, 8], [0, 16]], A.is_ge, 0, 1)
+    iota(V2("W1"), [[128, 16], [0, 128]], 0, 0, True)
+    iota(V2("p4"), [[1, 128]], 0, 0, True)
+    iota(V2("jc"), [[2, LC], [2 * LC, 16]], 0, 0, True)
+
+    def Z(name, i):
+        return V2(name, 15 - i, 143 - i)
+
+    for z in range(3):
+        act(V2("Vwin", 512 * z, 512 * z + 512), V2("rst"), scale=0.0)
+
+    cp(V2("I1"), V2("Id"))
+    ts(V2("I4"), V2("Id"), 4096.0, None, A.mult)
+    cp(V2("rkF", p=P8), V2("rkI", p=P8))
+    ts(V2("loI"), V2("sdI"), 4095, None, A.bitwise_and)
+    ts(V2("hiI"), V2("sdI"), 12, None, A.arith_shift_right)
+    mm(V2("b4", 0, 16), V2("Rm", p=P8), V2("rkF", p=P8), True, True)
+    cp(V2("loF"), V2("loI"))
+    cp(V2("hiF"), V2("hiI"))
+    ts(V2("Lr"), V2("iotaK"), V2("loF"), None, A.add)
+    ts(V2("hpF"), V2("hiI"), 64.0, -262144.0, A.mult, A.add)
+    ts(V2("Lq"), V2("Lr"), 4095, None, A.bitwise_and)
+    ts(V2("Hh"), V2("onef", 0, 64), V2("hiF"), -2048.0, A.mult, A.add)
+    tt(V2("b6", 0, 64), V2("Lq"), V2("Lq"), A.mult)
+    ts(V2("Lh"), V2("Lq"), -2048.0, None, A.add)
+    ts(V2("t1"), V2("b6", 0, 64), V2("hpF"), None, A.add)
+    ts(V2("Lp"), V2("Lq"), 64.0, -262144.0, A.mult, A.add)
+    ts(V2("Bq"), V2("t1"), 6, 4095, A.arith_shift_right, A.bitwise_and)
+    tt(V2("tA"), V2("w4c"), V2("b4", 0, 8), A.add)
+    tt(V2("b6", 64, 128), V2("Bq"), V2("Bq"), A.mult)
+    tt(V2("dA"), V2("b4", 8, 16), V2("w1c"), A.subtract)
+    tt(V2("t2"), V2("Lp"), V2("b6", 64, 128), A.add)
+    ts(V2("dB"), V2("dA"), -1.0, 1.0, A.mult, A.add)
+    ts(V2("w12"), V2("t2"), 3, 28672, A.arith_shift_right, A.bitwise_and)
+    tt(V2("Zk"), V2("w12"), V2("Bq"), A.add)
+
+    def spread(bank, us):
+        for j, u in enumerate(us):
+            o = V2(bank, 64 * j, 64 * j + 64)
+            mm(o, V2("I4", u, u + 128), V2("Lh"), True, False)
+            mm(o, V2("I1", u, u + 128), V2("Hh"), False, True)
+        for j, u in enumerate(us):
+            act(V2("VxS", u, 1024, 16, key="VxS%d" % u), V2(bank, 64 * j, 64 * j + 64))
+
+    act(V2("Id192"), V2("Id", 0, 128), scale=192.0)
+    spread("b0", range(0, 6))
+    own = V2("b3", 0, 64)
+    IdM = V2("Id", 0, 128)
+    k = 0
+    for w in range(8):
+        ts(V2("stp", 64 * k, 64 * k + 64), V2("Zk"), V2("tA", w, w + 1), V2("dA", w, w + 1), A.is_ge, A.mult)
+        k += 1
+        if w < 7:
+            ts(V2("stp", 64 * k, 64 * k + 64), V2("Zk"), 4096.0 * (w + 1), V2("dB", w, w + 1), A.is_ge, A.mult)
+            k += 1
+    for j in range(15):
+        mm(own, IdM, V2("stp", 64 * j, 64 * j + 64), j == 0, j == 14)
+    spread("b1", range(6, 11))
+    spread("b7", range(11, 16))
+    for s in range(N):
+        ts(V2("b2", 64 * s, 64 * s + 64), own, float(owner[s]), None, A.is_equal)
+    op("v", lambda: g.vector.tensor_tensor_scan(T.Pc[:], T.rst[:], T.b2[:], 0.0, A.mult, A.add), [V2("Pc")], [V2("rst"), V2("b2")])
+    cp(V2("ownb"), own)
+    tt(V2("Dc"), V2("Pc"), V2("b2"), A.mult)
+    cnt = V2("Pc", 63, 512, 64)
+    mm(V2("b4", 16, 24), V2("Tri"), cnt, True, True)
+    f2 = V2("b5", 0, 64)
+    mm(f2, V2("Id192"), V2("ownb"), True, False)
+    for s in range(N):
+        mm(f2, IdM, V2("Dc", 64 * s, 64 * s + 64), False, False)
+    for s in range(N):
+        ts(V2("Of", 64 * s, 64 * s + 64), V2("ownb"), float(owner[s]), V2("b4", 16 + s, 17 + s), A.is_equal, A.mult)
+        mm(f2, IdM, V2("Of", 64 * s, 64 * s + 64), False, s == N - 1)
+    ts(V2("ot"), V2("b4", 16, 24), -2.0, 1.0, A.mult, A.add)
+    cp((T.rnS[:, :, 1], [("rnS", 2 * s + 1, 2 * s + 2) for s in range(N)]), cnt)
+    ts(V2("F2u"), f2, -1.0, None, A.add)
+    tt((T.rnS[:, :, 0], [("rnS", 2 * s, 2 * s + 1) for s in range(N)]), V2("ot"), cnt, A.subtract)
+    send([(s, owner[s], V3("rnS", s, s + 1, 0, 2), T.rn[:, s, :]) for s in FAR], "rn")
+    aff(V2("Za"), V2("Zs"), [[-16, 9], [0, 16]], A.is_ge, 0, 1)
+    aff(V2("Zt"), V2("Za"), [[16, 9], [0, 16]], A.is_ge, 2, -1)
+    aff(V2("Zs"), V2("Za"), [[16, 9], [0, 16]], A.is_ge, 15, -1)
+    iota(V2("Ci"), [[0, 3], [2048, 3], [0, LC]], 0, 0, True)
+    aff(V2("Zb"), V2("Zs"), [[-16, 9], [0, 16]], A.is_ge, -3, 1)
+    aff(V2("Zi"), V2("Zb"), [[16, 9], [0, 16]], A.is_ge, 4, -1)
+
+    vxs = (T.VxS[:], [("VxS%d" % u, u, 1024) for u in range(16)])
+    cp(IX(V2("Vwin"), V2("F2u")), vxs)
+    for s in range(N):
+        q = owner[s]
+        dma("ys"[s % 2], V3("vl", s, s + 1, 0, LC), (T.Vwin[0:128:16, CAPQ * q:CAPQ * q + CAPQ], [("Vwin", CAPQ * q, CAPQ * q + CAPQ)]))
+
+    def piece(j):
+        dma("y", (T.W1[j:128:16, :], [("W1p%d" % j, 0, 2048)]), V2("p%d" % j), [("W1", 0, 2048)])
+
+    def pieces():
+        piece(4)
+        ts(V2("T0"), V2("thrI"), 4096.0, None, A.mult)
+        tt(V2("T1"), V2("T0"), V2("aliI"), A.add)
+        ts(V2("T2"), V2("T1"), 16777216.0, None, A.min)
+        cp(V2("p0"), V2("T2"))
+        tt(V2("r1"), V2("T2"), V2("p0"), A.subtract)
+        cp(V2("p1"), V2("r1"))
+        tt(V2("p2"), V2("r1"), V2("p1"), A.subtract)
+        for j in range(3):
+            piece(j)
+    tab = (T.W1[:], [("W1", 0, 2048)] + [("W1p%d" % j, 0, 2048) for j in (0, 1, 2, 4)])
+
+    def RN(s, k):
+        return V3("rnS" if s == S0 else "rn", s, s + 1, k, k + 1)
+
+    for s in range(N):
+        act(V2("ab", CAPQ * s, CAPQ * s + CAPQ), V2("jc"), F.Abs, bias=RN(s, 0))
+
+    def masks(a, b):
+        for s in range(a, b):
+            ts(V2("mk", CAPQ * s, CAPQ * s + CAPQ), V2("ab", CAPQ * s, CAPQ * s + CAPQ), RN(s, 1), float(2 ** (20 - asker[s])), A.is_lt, A.mult)
+
+    def ylist():
+        ts(V2("F2i"), f2, -1.0, None, A.add)
+        ts(V2("own176"), V2("ownb"), 176.0, None, A.mult)
+        ts(V2("own2k"), V2("ownb"), 2048.0, None, A.mult)
+        ts(V2("ya"), V2("F2i"), 10923.0, None, A.mult)
+        ts(V2("yc"), V2("F2i"), 16.0, None, A.mult)
+        ts(V2("yb"), V2("ya"), 17, None, A.arith_shift_right)
+        tt(V2("yc"), V2("yc"), V2("own176"), A.add)
+        ts(V2("yb"), V2("yb"), -191.0, None, A.mult)
+        tt(V2("yd"), V2("yb"), V2("yc"), A.add)
+        cp(V2("yo"), V2("yd"))
+
+    def hashes(c):
+        a, b = HS[c]
+
+        def W(nm):
+            return V3(nm, a, b, 0, 48)
+
+        def out(sem, src, dst):
+            for gr in GRP:
+                if a <= gr[0] < b:
+                    send([(s, owner[s], src(s), dst(s)) for s in gr], sem)
+        e = b if c == 0 else N
+        for i in range(4 if c < 2 else 0):
+            kk = ((1597 * (i + 1)) & 4095) - 4096
+            ts(V3("hx", a, e, LC * i, LC * i + LC), V3("vl", a, e, 0, LC), 4096.0 * kk + 2048.0 * 4097.0, None, A.add)
+        ts(W("hL"), W("hx"), 12, 4095, A.arith_shift_right, A.bitwise_and)
+        ts(W("h4"), W("hx"), 4095, None, A.bitwise_and)
+        tt(W("hq"), W("hL"), W("hL"), A.mult)
+        p = V2("b6", 48 * a, 48 * b)
+        ts(p, W("h4"), 64.0, -262144.0, A.mult, A.add)
+        tt(W("ht"), W("hq"), p, A.add)
+        ts(p, W("hL"), 64.0, -262144.0, A.mult, A.add)
+        ts(W("hB"), W("ht"), 6, 4095, A.arith_shift_right, A.bitwise_and)
+        tt(W("hb"), W("hB"), W("hB"), A.mult)
+        tt(W("hu"), W("hb"), p, A.add)
+        ts(p, W("hB"), 4096.0, 2048.0, A.mult, A.add)
+        ts(W("he"), W("hu"), 7, 2047, A.arith_shift_right, A.bitwise_and)
+        cp(V2("le", 48 * a, 48 * b), W("he"))
+        out("rl", lambda s: V2("le", 48 * s, 48 * s + 48), lambda s: T.rl[:, 48 * s:48 * s + 48])
+        tt(W("msg"), W("he"), p, A.add)
+        out("rq", lambda s: V3("msg", s, s + 1, 0, 48), lambda s: T.rq[:, s, :])
+
+    def look(c):
+        a, b = CH[c]
+        lst = "le" if a == S0 else "rl"
+        for s in range(a, b):
+            act(V2("GT", 768 * s, 768 * s + 768), IX(tab, V2(lst, 48 * s, 48 * s + 48)))
+
+    def arrive(c):
+        a, b = CH[c]
+        for i in range(16):
+            mm(V2(TB[c % 3], 0, 48 * (b - a)), Z("Zt", i), V2("GT", 768 * a + i, 768 * b, 16), i == 0, i == 15)
+
+    def filt(c):
+        a, b = CH[c]
+        tt(V3("mn", a, b, 0, 48), V3("msg" if a == S0 else "rq", a, b, 0, 48), V2(TB[c % 3], 0, 48 * (b - a)), A.min)
+        ts(V3("cI", a, b, 0, 48), V3("mn", a, b, 0, 48), 2047, None, A.bitwise_and)
+        cp(V2("ls", 36 * a, 36 * b), V3("cI", a, b, 0, 36))
+        for s in range(a, b):
+            for i in range(3):
+                o = 576 * s + CAPQ * i
+                tt(V2("MG", o, o + CAPQ), IX(V2("seenS"), V2("ls", 36 * s + LC * i, 36 * s + LC * i + LC)), V2("mk", CAPQ * s, CAPQ * s + CAPQ), A.mult)
+        o = V2("b%d" % (2 + c % 2), 0, 36 * (b - a))
+        mm(o, IdM, V2("Ci", 0, 36 * (b - a)), True, False)
+        for i in range(16):
+            mm(o, Z("Zs", i), V2("MG", 576 * a + i, 576 * b, 16), False, i == 15)
+        ts(V3("ky", a, b, 36, 48), V3("cI", a, b, 36, 48), 6144.0, None, A.add)
+
+    def pick(c):
+        a, b = CH[c]
+        cp(V2("sI", 36 * a, 36 * b), V2("b%d" % (2 + c % 2), 0, 36 * (b - a)))
+        ts(V3("sb", a, b, 0, 36), V2("sI", 36 * a, 36 * b), 2 ** 20 + 3 * 2048, None, A.bitwise_and)
+        tt(V3("ky", a, b, 0, 36), V3("sb", a, b, 0, 36), V3("cI", a, b, 0, 36), A.add)
+        tt(V3("m2", a, b, 0, 24), V3("ky", a, b, 0, 24), V3("ky", a, b, 24, 48), A.min)
+        x = (LC * a, LC * b)
+        tt(V2("kc", *x), V3("m2", a, b, 0, 12), V3("m2", a, b, 12, 24), A.min)
+        ts(V2("xI", *x), V2("kc", *x), 2047, None, A.bitwise_and)
+        cp(V2("lx", *x), V2("xI", *x))
+        if a == S0:
+            act(V2("land", CAPQ * me, CAPQ * me + CAPQ), IX(V2("vecS"), V2("lx", *x)))
+            return
+        act(V2("rs", CAPQ * a, CAPQ * b), IX(V2("vecS"), V2("lx", *x)))
+        for gr in GRP:
+            if a <= gr[0] < b:
+                send([(s, asker[s], V2("lx", LC * s, LC * s + LC), T.lr[:, LC * s:LC * s + LC]) for s in gr], "lr")
+                send([(s, asker[s], V2("rs", CAPQ * s, CAPQ * s + CAPQ), T.land[:, CAPQ * me:CAPQ * me + CAPQ]) for s in gr], "la")
+
+    def items(c):
+        for s in range(*CH[c]):
+            o = CAPQ * owner[s]
+            act(V2("IDx", o, o + CAPQ), IX(tab, V2("lx" if s == S0 else "lr", LC * s, LC * s + LC)))
+
+    BLOCK = {"H": hashes, "G": look, "A": arrive, "F": filt, "P": pick, "I": items, "Y": ylist, "M": masks, "T": pieces}
+    for blocks in PLAN:
+        turns = []
+        for n, (k, f, *y) in enumerate(blocks):
+            stream[0] = []
+            BLOCK[f](*y)
+            started = False
+            for (q, h) in stream[0]:
+                k += 1 if q == "v" and started else 0
+                started = True
+                turns.append((k, n, len(turns), h))
+        stream[0] = None
+        for x in sorted(turns, key=lambda x: x[:3]):
+            x[3]()
+
+    def ygat(h):
+        return V2("yS", 512 * h, 512 * h + 512), IX(V2("land"), V2("yo", 32 * h, 32 * h + 32))
+
+    def igat(h):
+        return V2("IDg", 512 * h, 512 * h + 512), IX(V2("IDx"), V2("yo", 32 * h, 32 * h + 32))
+    act(*igat(1))
+    cp(*igat(0))
+    cp(*ygat(0))
+    dma("y", hbm(T.y[:, 0:512]), V2("yS", 0, 512))
+    act(*ygat(1))
+    for i in range(16):
+        mm(V2("b4", 64, 128), Z("Zi", i), V2("IDg", i, 1024, 16), i == 0, i == 15)
+    tt(V2("chS"), V2("own2k"), V2("b4", 64, 128), A.add)
+    dma("s", hbm(T.y[:, 512:1024]), V2("yS", 512, 1024))
+    dma("s", hbm(T.chosen[:]), V2("chS"))
+
+    for s, n in count.items():
+        if clock["g"].get(s, 0) < n:
+            g.wait_ge(T.sem[s], n)

@@ -4,40 +4,46 @@ from concourse.mybir import AluOpType, ActivationFunctionType
 A = AluOpType
 F = ActivationFunctionType
 N = 8
-CAPQ, LC = 192, 12
-S0 = N - 1
-HS = [(0, 2), (2, 4), (4, 8)]
+CAPQ, LC, SW = 192, 12, 256
+S0 = 7
 CH = [(0, 2), (2, 4), (4, 6), (6, 7), (7, 8)]
 GRP = [(0, 1), (2, 3), (4, 5), (6,)]
-PLAN = [[(0, "T")],
-        [(0, "H", 0), (7, "H", 1), (24, "G", 0), (24, "A", 0), (25, "G", 1), (20, "H", 2), (22, "M", 0, 4), (34, "A", 1), (34, "G", 2)],
-        [(0, "F", 0), (0, "M", 4, 8), (1, "G", 3), (9, "A", 2), (8, "F", 1), (13, "P", 0), (17, "A", 3), (20, "G", 4), (16, "F", 2), (21, "P", 1), (25, "A", 4),
-         (24, "F", 3), (27, "P", 2), (34, "I", 0), (30, "F", 4), (33, "P", 3), (40, "I", 1), (40, "P", 4), (39, "Y"), (52, "I", 4), (53, "I", 2), (54, "I", 3)]]
+ORDER = [4, 0, 1, 2, 3]
+DUE = [(16.2, 13.7), (14.1, 11.5), (11.8, 9.4), (10.7, 8.5), (18.4, 8.0)]
+COST = {"cycle": 0.0009, "gather": 0.0013, "scatter": 0.0025, "mm": 0.0007, "wait": 0.2, "dma": 0.06, "load": 1.3, "byte": 0.0005, "call": 0.4, "far": 1.8, "first": 2.0, "link": 1.0}
+AHEAD, TURNS = 0.2, 1
+SOON = {"rn": 6.0, "W1": 3.0}
+MGW = 36
+PARTS = 2
+ROW = 1 << 16
+GV = (1,)
 TB = ["b0", "b1", "b7"]
 f32, b16, i32, u16, f16 = "float32", "bfloat16", "int32", "uint16", "float16"
 SHAPES = {
-    i32: {"sdI": 1, "rkI": 16, "thrI": 128, "aliI": 128, "iotaK": 64,
-          "loI": 1, "hiI": 1, "Lr": 64, "Lq": 64, "t1": 64, "Bq": 64, "Lp": 64, "t2": 64, "w12": 64,
-          "F2i": 64, "ya": 64, "yb": 64, "yc": 64, "yd": 64, "own176": 64,
-          "hx": (8, 48), "hL": (8, 48), "h4": (8, 48), "hq": (8, 48), "ht": (8, 48), "hB": (8, 48), "hb": (8, 48), "hu": (8, 48), "he": (8, 48),
-          "mn": (8, 48), "cI": (8, 48), "sI": 288, "sb": (8, 36), "ky": (8, 48), "m2": (8, 24), "kc": 96, "xI": 96},
-    f32: {"rkF": 16, "onef": 128, "Rm": 128, "w1c": 8, "w4c": 8, "loF": 1, "hiF": 1, "hpF": 1, "Zk": 64, "tA": 8, "dA": 8, "dB": 8,
-          "VxS": 1024, "Vwin": 1536, "vl": (8, 12), "own2k": 64, "ot": 8, "T0": 128, "T1": 128, "T2": 128, "r1": 128,
-          "rnS": (8, 2), "rn": (8, 2), "msg": (8, 48), "rq": (8, 48), "chS": 64},
-    b16: {"seenS": 2048, "vecS": 2048, "W1": 2048, "oneb": 144, "Id": 144, "Id192": 128, "Tri": 128, "rst": 512, "Ci": 108,
-          "Zs": 144, "Za": 144, "Zb": 144, "Zt": 144, "Zi": 144, "jc": 192, "stp": 1024, "Pc": 512, "Dc": 512, "Of": 512, "ownb": 64,
-          "p0": 128, "p1": 128, "p2": 128, "p4": 128, "rs": 1536, "land": 1536, "ab": 1536, "mk": 1536, "GT": 6144, "MG": 4608,
-          "IDx": 1536, "IDg": 1024, "yS": 1024},
-    u16: {"F2u": 64, "yo": 64, "le": 384, "rl": 384, "lx": 96, "lr": 96, "ls": 288},
-    f16: {"I1": 144, "I4": 144, "Lh": 64, "Hh": 64},
+    i32: {"sdI": 1, "rkI": 16, "thrI": 128, "aliI": 128, "iotaK": 64, "pI": 1, "pm": 1, "pg": 1,
+          "loI": 1, "hiI": 1, "Lr": 64, "Lq": 64, "t1": 64, "Bq": 64, "Lp": 64, "t2": 64, "w12": 64, "fh": 64,
+          "hx": 256, "hL": 256, "ht": 256, "hB": 256, "hu": 256, "he": 256,
+          "mn": (8, 48), "cI": (96, 4), "sI": (96, 4), "sb": 384},
+    f32: {"rkF": 16, "BDf": 128, "w1c": 8, "w4c": 8, "sdF": 1, "pgF": 1, "iotaC": 256, "hpF": 1, "Zk": 64, "tA": 8, "dA": 8, "dB": 8,
+          "pmF": 1, "cxF": 1, "nC": 256, "loC": 1, "hiC": 1, "hv": 512, "fa": 64, "Lf": 256, "Bf": 256, "hq": 256, "hb": 256,
+          "VxS": 1024, "Vwin": 2048, "own2k": 64, "T0": 128, "T1": 128,
+          "msg": (8, 48), "rq": (8, 48), "chS": 64, "ka": 384, "kb": 384, "kc": 384},
+    b16: {"seenS": 2048, "vecS": 2048, "W1": 2048, "oneb": 256, "gC": 128, "Gc": 128, "Id": 128, "Tri": 128, "BD": 128, "rst": 512, "uC": 256, "s256": 8,
+          "Zs": 144, "Za": 144, "Zt": 144, "Zi": 144, "jc": 576, "stp": 1024, "Pc": 512, "Dc": 512, "ownb": 64,
+          "p0": 128, "p1": 128, "p2": 128, "p4": 128, "rs": 1536, "land": 2048, "seenD": 2048, "Md": 128, "rnS": (8, 2), "rn": (8, 2), "mk": 4608, "GT": 6144, "MG": 4608,
+          "IDx": 2048, "IDg": 1024, "yS": 1024},
+    u16: {"F2u": 64, "yo": 64, "le": (8, 48), "rl": 384, "lx": 96, "lr": 96, "ls": 288},
+    f16: {"I1": 128, "G1": 128, "G64": 128, "Rlo": 256, "Rhi": 256, "Of": 512},
 }
+for _v in range(8):
+    SHAPES[f32]["fv%d" % _v] = (8, 16)
 SCRATCH = {}
 for _dt, _d in SHAPES.items():
     for _k, _n in _d.items():
         SCRATCH[_k] = ("sbuf", [128] + (list(_n) if isinstance(_n, tuple) else [_n]), _dt)
 for _b in range(8):
     SCRATCH["b%d" % _b] = ("psum", [128, 512], f32)
-SEMAPHORES = ["sv", "ss", "st", "sg", "lsem"] + ["d%d" % _k for _k in range(32)] + ["%s%d" % (_m, _k) for _m in ("rn", "rl", "rq", "lr", "la") for _k in range(N)]
+SEMAPHORES = ["sv", "ss", "st", "sg", "lsem"] + ["d%d" % _k for _k in range(40)] + ["%s%d" % (_m, _k) for _m in ("rn", "rl", "rq", "lr", "la") for _k in range(N)]
 
 
 def rank_program(g, core, T, topo):
@@ -51,25 +57,36 @@ def rank_program(g, core, T, topo):
     log = {}
     ndma = [0]
 
-    def V2(name, a=0, b=None, step=1, p=None, key=None):
+    def V2(name, a=0, b=None, step=1, p=None):
         b = SCRATCH[name][1][1] if b is None else b
         ap = T[name][:, a:b:step] if p is None else T[name][p, a:b:step]
-        return (ap, [(key or name, a, b)])
+        return (ap, [(name, a, b)], len(range(a, b, step)))
 
     def V3(name, s0, s1, a, b):
         w = SCRATCH[name][1][2]
         ap = T[name][:, s0, a:b] if s1 == s0 + 1 else T[name][:, s0:s1, a:b]
-        return (ap, [(name, s * w + a, s * w + b) for s in range(s0, s1)])
+        return (ap, [(name, s * w + a, s * w + b) for s in range(s0, s1)], (s1 - s0) * (b - a))
+
+    def E(name, s0, s1, a, b):
+        w = SCRATCH[name][1][2]
+        ap = T[name][:, LC * s0:LC * s1, a] if b == a + 1 else T[name][:, LC * s0:LC * s1, a:b]
+        return (ap, [(name, s * w + a, s * w + b) for s in range(s0, s1)], (s1 - s0) * LC * (b - a))
 
     def IX(win, off):
-        return (win[0].indirect(off[0]), win[1] + off[1])
+        return (win[0].indirect(off[0]), win[1] + off[1], 16 * off[2], True)
+
+    def row(nm, v):
+        return (T[nm][v:128:16, :], [(nm, ROW + v, ROW + v + 1)], SCRATCH[nm][1][1] // 16)
+
+    def rows(nm):
+        return (T[nm][:], [(nm, 0, ROW + 16)], SCRATCH[nm][1][1])
 
     BANKS = ["b%d" % k for k in range(8)]
 
     def need(q, reads, writes):
         toks = []
-        for regs, w in ((reads, False), (writes, True)):
-            for (k, lo, hi) in regs:
+        for rs, w in ((reads, False), (writes, True)):
+            for (k, lo, hi) in rs:
                 for (l2, h2, w2, tok, e2) in log.get(k, []):
                     if k in BANKS and e2 != q:
                         toks.append(tok)
@@ -94,26 +111,95 @@ def rank_program(g, core, T, topo):
         c = dict(clock[q])
         c[sem] = count[sem]
         seen_by[tok] = c
-        for regs, w in ((reads, False), (writes, True)):
-            for (k, lo, hi) in regs:
+        for rs, w in ((reads, False), (writes, True)):
+            for (k, lo, hi) in rs:
                 log.setdefault(k, []).append((lo, hi, w, tok, q))
 
-    stream = [None]
+    calls = []
+    moved, soon, due, LINK = {}, {}, {}, ("link", 0, 1)
 
-    def later(q, f):
-        if stream[0] is None:
-            f()
-        else:
-            stream[0].append((q, f))
+    def regs(views):
+        return [r for x in views for r in x[1]]
 
     def now(q, f, outs, ins):
-        reads = [r for x in ins for r in x[1]]
-        writes = [r for x in outs for r in x[1]]
-        need(q, reads, writes)
-        done(q, f(), reads, writes, "s" + q, 1)
+        need(q, regs(ins), regs(outs))
+        done(q, f(), regs(ins), regs(outs), "s" + q, 1)
 
-    def op(q, f, outs, ins):
-        later(q, lambda: now(q, f, outs, ins))
+    def wide(x):
+        return SCRATCH[x[1][0][0]][2] in (f32, i32)
+
+    def op(q, f, outs, ins, cyc=1.0):
+        n = outs[0][2]
+        if len(outs[0]) > 3:
+            t = 0.05 + COST["scatter"] * ins[0][2]
+        elif ins and len(ins[0]) > 3:
+            t = 0.06 + COST["gather"] * n
+        elif q == "t":
+            t = COST["mm"] * max(64, n) * (4 if wide(ins[0]) else 1)
+        elif q == "g":
+            t = 0.15 + 2 * COST["cycle"] * n
+        else:
+            t = COST["cycle"] * max(64, n * cyc * (0.5 if q == "v" and not any(wide(x) for x in outs + ins) else 1))
+        calls.append((q, lambda: now(q, f, outs, ins), regs(ins), regs(outs), t, COST["wait"]))
+
+    def issue():
+        touched, before = {}, []
+        for j, (q, f, reads, writes, t, lat) in enumerate(calls):
+            dep = set()
+            for rs, w in ((reads, False), (writes, True)):
+                for (k, lo, hi) in rs:
+                    dep |= {i for (l2, h2, w2, i) in touched.get(k, []) if (l2 < hi and lo < h2 and (w or w2)) or (k in BANKS and q == "t" == calls[i][0])}
+            before.append(dep)
+            for rs, w in ((reads, False), (writes, True)):
+                for (k, lo, hi) in rs:
+                    touched.setdefault(k, []).append((lo, hi, w, j))
+        after = [[] for c in calls]
+        for j, dep in enumerate(before):
+            for i in dep:
+                after[i].append(j)
+
+        def gap(i, j, early=0):
+            if LINK in calls[i][3] and LINK in calls[j][3]:
+                return COST["link"]
+            return 0.0 if calls[i][0] == calls[j][0] == "t" else calls[i][5] + moved.get(i, 0.0) + early * soon.get(i, 0.0)
+        banks = [{k for (k, lo, hi) in c[2] + c[3] if k in BANKS} for c in calls]
+
+        def deal(way, before, after, back):
+            left = [len(d) for d in before]
+            ready = {j: gap(j, j) if back else 0.0 for j in range(len(calls)) if not left[j]}
+            free = {q: 0.0 for q in list(queue) + ["dma"]}
+            bank, late, order, end = {}, {}, [], [0.0] * len(calls)
+            while ready:
+                st = {j: max([ready[j], free[calls[j][0]]] + [bank[k][1] for k in banks[j] if k in bank and bank[k][0] != calls[j][0]]) for j in ready}
+                first = min(ready, key=lambda j: (st[j], -way[j], j))
+                j = min((i for i in ready if calls[i][0] == calls[first][0] and st[i] <= st[first] + min(AHEAD * calls[first][4], 0.5)), key=lambda i: (-way[i], i))
+                q = calls[j][0]
+                order.append(j)
+                free[q] = end[j] = st[j] + calls[j][4]
+                held = 0.0
+                if j in moved and not back:
+                    held = max(0.0, free["dma"] - free[q])
+                    free["dma"] = free[q] + held + moved[j]
+                for k in banks[j]:
+                    bank[k] = (q, free[q] + COST["wait"])
+                del ready[j]
+                for k in after[j]:
+                    left[k] -= 1
+                    late[k] = max(late.get(k, 0.0), free[q] + held + (gap(k, j, 1) if back else gap(j, k)))
+                    if not left[k]:
+                        ready[k] = late[k]
+            return order, end
+        way = [0.0] * len(calls)
+        for j in reversed(range(len(calls))):
+            way[j] = calls[j][4] + max([gap(j, k, 1) + way[k] for k in after[j]] + [calls[j][5], due.get(j, 0.0)])
+        best = None
+        for turn in range(TURNS):
+            order, end = deal(way, before, after, False)
+            if best is None or max(end) < best[0]:
+                best = (max(end), order)
+            way = deal(end, after, before, True)[1]
+        for j in best[1]:
+            calls[j][1]()
 
     def isv(x):
         return isinstance(x, tuple)
@@ -129,7 +215,11 @@ def rank_program(g, core, T, topo):
             op("v", lambda: g.vector.tensor_scalar(out[0], in0[0], raw(s1), raw(s2), o0, o1), [out], ins)
 
     def tt(out, a, b, o):
-        op("v", lambda: g.vector.tensor_tensor(out[0], a[0], b[0], o), [out], [a, b])
+        cyc = 1 if a[1][0][0] in BANKS or b[1][0][0] in BANKS else 2 if wide(out) or wide(a) or wide(b) else 4
+        op("v", lambda: g.vector.tensor_tensor(out[0], a[0], b[0], o), [out], [a, b], cyc)
+
+    def scan(out, a, b, o0, o1):
+        op("v", lambda: g.vector.tensor_tensor_scan(out[0], a[0], b[0], 0.0, o0, o1), [out], [a, b])
 
     def cp(out, a):
         op("v", lambda: g.vector.tensor_copy(out[0], a[0]), [out], [a])
@@ -145,12 +235,19 @@ def rank_program(g, core, T, topo):
     def mm(out, lhs, rhs, start, stop):
         op("t", lambda: g.tensor.matmul(out[0], lhs[0], rhs[0], start, stop), [out], [lhs, rhs])
 
+    def back(out, z, src, a, b):
+        def run():
+            for i in range(16):
+                lhs, rhs = V2(z, 15 - i, 143 - i), V2(src, a + i, b, 16)
+                now("t", lambda: g.tensor.matmul(out[0], lhs[0], rhs[0], i == 0, i == 15), [out], [lhs, rhs])
+        calls.append(("t", run, V2(z)[1] + V2(src, a, b)[1], out[1], 16 * COST["mm"] * max(64, out[2]), COST["wait"]))
+
     def aff(out, a, pat, cmp, base, cm):
         op("g", lambda: g.affine_select(out[0], a[0], pat, cmp, 0.0, base, cm), [out], [a])
 
-    def iota(out, pat, base, cm, small=False):
+    def iota(out, pat, base, cm, small=False, after=()):
         if small:
-            op("g", lambda: g.iota(out[0], pat, base, cm, allow_small_or_imprecise_dtypes=True), [out], [])
+            op("g", lambda: g.iota(out[0], pat, base, cm, allow_small_or_imprecise_dtypes=True), [out], list(after))
         else:
             op("g", lambda: g.iota(out[0], pat, base, cm), [out], [])
 
@@ -161,10 +258,13 @@ def rank_program(g, core, T, topo):
         done(q, queue[q].dma_start(out[0], a[0]), a[1], out[1], sem, 16)
 
     def dma(q, out, a, after=()):
-        later(q, lambda: dma_now(q, out, a, list(after)))
+        size = max(out[2] * (4 if out[1] and wide(out) else 2), a[2] * (4 if a[1] and wide(a) else 2))
+        moved[len(calls)] = COST["byte"] * size
+        soon[len(calls)] = SOON.get(out[1][0][0], 0.0) if out[1] else 0.0
+        calls.append((q, lambda: dma_now(q, out, a, list(after)), a[1] + list(after), out[1], COST["dma"], COST["load"]))
 
     def hbm(ap):
-        return (ap, [])
+        return (ap, [], 0)
 
     def send_now(pairs, sem):
         need("g", [r for x in pairs for r in x[2][1]], [])
@@ -182,13 +282,18 @@ def rank_program(g, core, T, topo):
         g.remote_dma_fused(tr, local_sem=T.sem.lsem)
 
     def send(pairs, sem):
-        later("g", lambda: send_now(pairs, sem))
+        size = len(pairs) * pairs[0][2][2] * (4 if wide(pairs[0][2]) else 2)
+        moved[len(calls)] = 2 * COST["byte"] * size
+        soon[len(calls)] = SOON.get(sem, 0.0)
+        calls.append(("g", lambda: send_now(pairs, sem), regs([x[2] for x in pairs]), regs([LAND[sem](x[0]) for x in pairs]) + [LINK] * (sem == "la"),
+                      COST["call"] + (COST["first"] if sem == "rn" else 0), COST["far"]))
 
     def hops(d):
         a, b = topo.chip(T.cores[0]), topo.chip(T.cores[d])
-        return 3 if d == 0 else 2 if topo.mates(a, b) else 1 if topo.same_plane(a, b) else 0
+        return 2 if topo.mates(a, b) else 1 if topo.same_plane(a, b) else 0
 
-    DIST = sorted(range(N), key=hops)
+    DIST = sorted(range(1, N), key=hops)
+    DIST.insert(S0, 0)
     owner = [me ^ d for d in DIST]
     asker = owner
     FAR = [s for s in range(N) if s != S0]
@@ -201,259 +306,241 @@ def rank_program(g, core, T, topo):
         for (k, lo, hi) in view[1]:
             log.setdefault(k, []).append((lo, hi, True, (name, n), "remote"))
 
+    LAND = {"rn": lambda s: V3("rn", s, s + 1, 0, 2), "rl": lambda s: V2("rl", 48 * s, 48 * s + 48), "rq": lambda s: V3("rq", s, s + 1, 0, 48),
+            "lr": lambda s: V2("lr", LC * s, LC * s + LC), "la": lambda s: V2("land", SW * s, SW * s + CAPQ)}
     for s in FAR:
-        k = [len(gr) for gr in GRP if s in gr][0]
-        arrives("rn", s, asker[s], V3("rn", s, s + 1, 0, 2), N - 1)
-        arrives("rl", s, asker[s], V2("rl", 48 * s, 48 * s + 48), k)
-        arrives("rq", s, asker[s], V3("rq", s, s + 1, 0, 48), k)
-        arrives("lr", s, owner[s], V2("lr", LC * s, LC * s + LC), k)
-        arrives("la", s, owner[s], V2("land", CAPQ * owner[s], CAPQ * owner[s] + CAPQ), k)
+        for m in LAND:
+            arrives(m, s, asker[s], LAND[m](s), N - 1 if m == "rn" else [len(gr) for gr in GRP if s in gr][0])
 
     dma("y", V2("sdI"), hbm(T.sd[:]))
-    dma("s", V2("rkI", p=slice(0, 8)), hbm(T.rk[:]))
-    dma("y", V2("thrI"), hbm(T.thr[:]))
-    dma("s", V2("aliI"), hbm(T.ali[:]))
-    dma("y", V2("seenS"), hbm(T.seen[:]))
-    dma("y", V2("vecS"), hbm(T.vec[:]))
+    fill(V2("rkI"), 0)
+    dma("s", V2("rkI", p=slice(0, 128, 16)), hbm(T.rk[:]))
+    dma("y", V2("thrI"), hbm(T.thr[:]), V2("sdI")[1])
+    dma("y", V2("aliI"), hbm(T.ali[:]), V2("sdI")[1])
+    dma("y", V2("seenS"), hbm(T.seen[:]), V2("rkI")[1])
+    dma("y", V2("vecS"), hbm(T.vec[:]), V2("rkI")[1])
 
     fill(V2("oneb"), 1.0)
-    fill(V2("onef"), 1.0)
     fill(V2("rst"), 1.0)
+    iota(V2("pI"), [[0, 1]], 0, 1)
+    iota(V2("iotaK"), [[5 * 1597 - 8192, 64]], 0, 0)
+    iota(V2("gC"), [[1, 8], [0, 16]], 0, 0, True)
+    ts(V2("pg"), V2("pI"), 4, None, A.arith_shift_right)
+    cp(V2("pgF"), V2("pg"))
+    for nm, c in (("G1", 1.0), ("G64", 64.0), ("BDf", 1.0), ("BD", 1.0)):
+        ts(V2(nm), V2("gC"), V2("pgF"), c, A.is_equal, A.mult)
+    act(V2("Gc"), V2("BD"), scale=-8192.0)
+    iota(V2("uC", 0, 256 // PARTS), [[0, 16 // PARTS], [1, 16]], 0, 0, True)
+    iota(V2("w1c"), [[1, 8]], 0, 0, True)
+    iota(V2("iotaC"), [[1597, 4], [7985, 4], [0, 16]], 1597 + 2048, 0, True)
+    aff(V2("Id"), V2("oneb", 0, 128), [[-1, 128]], A.is_equal, 0, 1)
+    aff(V2("Tri"), V2("BD"), [[1, 128]], A.is_gt, 0, -1)
+    iota(V2("W1"), [[128, 16], [0, 128]], 0, 0, True)
     fill(V2("rst", 0, 512, 64), 0.0)
     fill(V2("Zs"), 0.0)
+    ts(V2("pm"), V2("pI"), 15, None, A.bitwise_and)
     fill(V2("Zs", 15, 144, 16), 1.0)
-    iota(V2("iotaK"), [[7985, 64]], 0, 0)
-    iota(V2("w1c"), [[1, 8]], 0, 0, True)
-    iota(V2("w4c"), [[4096, 8]], 0, 0, True)
-    P8 = slice(0, 8)
-    aff(V2("Id"), V2("oneb"), [[-1, 144]], A.is_equal, 0, 1)
-    aff(V2("Rm", p=P8), V2("onef", 0, 128, p=P8), [[1, 128]], A.is_ge, 0, -16)
-    aff(V2("Rm", p=P8), V2("Rm", p=P8), [[-1, 128]], A.is_ge, 15, 16)
-    aff(V2("Tri"), V2("oneb", 0, 128), [[16, 8], [1, 16]], A.is_gt, 0, -1)
-    aff(V2("Tri"), V2("Tri"), [[-16, 8], [0, 16]], A.is_ge, 0, 1)
-    iota(V2("W1"), [[128, 16], [0, 128]], 0, 0, True)
-    iota(V2("p4"), [[1, 128]], 0, 0, True)
-    iota(V2("jc"), [[2, LC], [2 * LC, 16]], 0, 0, True)
+    cp(V2("pmF"), V2("pm"))
+    ts(V2("cxF"), V2("pm"), 4.0 * 7985.0, None, A.mult)
 
-    def Z(name, i):
-        return V2(name, 15 - i, 143 - i)
-
-    for z in range(3):
-        act(V2("Vwin", 512 * z, 512 * z + 512), V2("rst"), scale=0.0)
-
-    cp(V2("I1"), V2("Id"))
-    ts(V2("I4"), V2("Id"), 4096.0, None, A.mult)
-    cp(V2("rkF", p=P8), V2("rkI", p=P8))
+    for nm, n in (("VxS", 2), ("Vwin", 4)):
+        for z in range(n):
+            act(V2(nm, 512 * z, 512 * z + 512), V2("rst"), scale=0.0)
     ts(V2("loI"), V2("sdI"), 4095, None, A.bitwise_and)
     ts(V2("hiI"), V2("sdI"), 12, None, A.arith_shift_right)
-    mm(V2("b4", 0, 16), V2("Rm", p=P8), V2("rkF", p=P8), True, True)
-    cp(V2("loF"), V2("loI"))
-    cp(V2("hiF"), V2("hiI"))
-    ts(V2("Lr"), V2("iotaK"), V2("loF"), None, A.add)
-    ts(V2("hpF"), V2("hiI"), 64.0, -262144.0, A.mult, A.add)
-    ts(V2("Lq"), V2("Lr"), 4095, None, A.bitwise_and)
-    ts(V2("Hh"), V2("onef", 0, 64), V2("hiF"), -2048.0, A.mult, A.add)
-    tt(V2("b6", 0, 64), V2("Lq"), V2("Lq"), A.mult)
-    ts(V2("Lh"), V2("Lq"), -2048.0, None, A.add)
-    ts(V2("t1"), V2("b6", 0, 64), V2("hpF"), None, A.add)
-    ts(V2("Lp"), V2("Lq"), 64.0, -262144.0, A.mult, A.add)
-    ts(V2("Bq"), V2("t1"), 6, 4095, A.arith_shift_right, A.bitwise_and)
-    tt(V2("tA"), V2("w4c"), V2("b4", 0, 8), A.add)
-    tt(V2("b6", 64, 128), V2("Bq"), V2("Bq"), A.mult)
-    tt(V2("dA"), V2("b4", 8, 16), V2("w1c"), A.subtract)
-    tt(V2("t2"), V2("Lp"), V2("b6", 64, 128), A.add)
-    ts(V2("dB"), V2("dA"), -1.0, 1.0, A.mult, A.add)
-    ts(V2("w12"), V2("t2"), 3, 28672, A.arith_shift_right, A.bitwise_and)
-    tt(V2("Zk"), V2("w12"), V2("Bq"), A.add)
 
-    def spread(bank, us):
-        for j, u in enumerate(us):
-            o = V2(bank, 64 * j, 64 * j + 64)
-            mm(o, V2("I4", u, u + 128), V2("Lh"), True, False)
-            mm(o, V2("I1", u, u + 128), V2("Hh"), False, True)
-        for j, u in enumerate(us):
-            act(V2("VxS", u, 1024, 16, key="VxS%d" % u), V2(bank, 64 * j, 64 * j + 64))
-
-    act(V2("Id192"), V2("Id", 0, 128), scale=192.0)
-    spread("b0", range(0, 6))
     own = V2("b3", 0, 64)
-    IdM = V2("Id", 0, 128)
-    k = 0
-    for w in range(8):
-        ts(V2("stp", 64 * k, 64 * k + 64), V2("Zk"), V2("tA", w, w + 1), V2("dA", w, w + 1), A.is_ge, A.mult)
-        k += 1
-        if w < 7:
-            ts(V2("stp", 64 * k, 64 * k + 64), V2("Zk"), 4096.0 * (w + 1), V2("dB", w, w + 1), A.is_ge, A.mult)
-            k += 1
-    for j in range(15):
-        mm(own, IdM, V2("stp", 64 * j, 64 * j + 64), j == 0, j == 14)
-    spread("b1", range(6, 11))
-    spread("b7", range(11, 16))
-    for s in range(N):
-        ts(V2("b2", 64 * s, 64 * s + 64), own, float(owner[s]), None, A.is_equal)
-    op("v", lambda: g.vector.tensor_tensor_scan(T.Pc[:], T.rst[:], T.b2[:], 0.0, A.mult, A.add), [V2("Pc")], [V2("rst"), V2("b2")])
-    cp(V2("ownb"), own)
-    tt(V2("Dc"), V2("Pc"), V2("b2"), A.mult)
-    cnt = V2("Pc", 63, 512, 64)
-    mm(V2("b4", 16, 24), V2("Tri"), cnt, True, True)
+    IdM = V2("Id")
     f2 = V2("b5", 0, 64)
-    mm(f2, V2("Id192"), V2("ownb"), True, False)
-    for s in range(N):
-        mm(f2, IdM, V2("Dc", 64 * s, 64 * s + 64), False, False)
-    for s in range(N):
-        ts(V2("Of", 64 * s, 64 * s + 64), V2("ownb"), float(owner[s]), V2("b4", 16 + s, 17 + s), A.is_equal, A.mult)
-        mm(f2, IdM, V2("Of", 64 * s, 64 * s + 64), False, s == N - 1)
-    ts(V2("ot"), V2("b4", 16, 24), -2.0, 1.0, A.mult, A.add)
-    cp((T.rnS[:, :, 1], [("rnS", 2 * s + 1, 2 * s + 2) for s in range(N)]), cnt)
-    ts(V2("F2u"), f2, -1.0, None, A.add)
-    tt((T.rnS[:, :, 0], [("rnS", 2 * s, 2 * s + 1) for s in range(N)]), V2("ot"), cnt, A.subtract)
-    send([(s, owner[s], V3("rnS", s, s + 1, 0, 2), T.rn[:, s, :]) for s in FAR], "rn")
-    aff(V2("Za"), V2("Zs"), [[-16, 9], [0, 16]], A.is_ge, 0, 1)
-    aff(V2("Zt"), V2("Za"), [[16, 9], [0, 16]], A.is_ge, 2, -1)
-    aff(V2("Zs"), V2("Za"), [[16, 9], [0, 16]], A.is_ge, 15, -1)
-    iota(V2("Ci"), [[0, 3], [2048, 3], [0, LC]], 0, 0, True)
-    aff(V2("Zb"), V2("Zs"), [[-16, 9], [0, 16]], A.is_ge, -3, 1)
-    aff(V2("Zi"), V2("Zb"), [[16, 9], [0, 16]], A.is_ge, 4, -1)
+    cnt = V2("Pc", 63, 512, 64)
 
-    vxs = (T.VxS[:], [("VxS%d" % u, u, 1024) for u in range(16)])
-    cp(IX(V2("Vwin"), V2("F2u")), vxs)
-    for s in range(N):
-        q = owner[s]
-        dma("ys"[s % 2], V3("vl", s, s + 1, 0, LC), (T.Vwin[0:128:16, CAPQ * q:CAPQ * q + CAPQ], [("Vwin", CAPQ * q, CAPQ * q + CAPQ)]))
+    def owners():
+        cp(V2("sdF"), V2("sdI"))
+        ts(V2("hpF"), V2("hiI"), 64.0, -262144.0, A.mult, A.add)
+        ts(V2("Lr"), V2("iotaK"), V2("sdF"), None, A.add)
+        cp(V2("rkF"), V2("rkI"))
+        ts(V2("Lq"), V2("Lr"), 4095, None, A.bitwise_and)
+        mm(V2("b4", 0, 16), V2("BDf"), V2("rkF"), True, True)
+        tt(V2("b6", 0, 64), V2("Lq"), V2("Lq"), A.mult)
+        act(V2("w4c"), V2("w1c"), scale=4096.0)
+        ts(V2("t1"), V2("b6", 0, 64), V2("hpF"), None, A.add)
+        ts(V2("Lp"), V2("Lq"), 64.0, -262144.0, A.mult, A.add)
+        ts(V2("Bq"), V2("t1"), 6, 4095, A.arith_shift_right, A.bitwise_and)
+        tt(V2("tA"), V2("w4c"), V2("b4", 0, 8), A.add)
+        tt(V2("b6", 64, 128), V2("Bq"), V2("Bq"), A.mult)
+        tt(V2("dA"), V2("b4", 8, 16), V2("w1c"), A.subtract)
+        tt(V2("t2"), V2("Lp"), V2("b6", 64, 128), A.add)
+        ts(V2("dB"), V2("dA"), -1.0, 1.0, A.mult, A.add)
+        ts(V2("w12"), V2("t2"), 3, 28672, A.arith_shift_right, A.bitwise_and)
+        act(V2("s256"), V2("w1c"), scale=float(SW))
+        tt(V2("Zk"), V2("w12"), V2("Bq"), A.add)
+        cp(V2("I1"), V2("Id"))
+        k = 0
+        for w in range(8):
+            ts(V2("stp", 64 * k, 64 * k + 64), V2("Zk"), V2("tA", w, w + 1), V2("dA", w, w + 1), A.is_ge, A.mult)
+            mm(own, IdM, V2("stp", 64 * k, 64 * k + 64), k == 0, k == 14)
+            k += 1
+            if w < 7:
+                ts(V2("stp", 64 * k, 64 * k + 64), V2("Zk"), 4096.0 * (w + 1), V2("dB", w, w + 1), A.is_ge, A.mult)
+                mm(own, IdM, V2("stp", 64 * k, 64 * k + 64), False, False)
+                k += 1
+        for s in range(N):
+            ts(V2("b2", 64 * s, 64 * s + 64), own, float(owner[s]), None, A.is_equal)
+        scan(V2("Pc"), V2("rst"), V2("b2"), A.mult, A.add)
+        cp(V2("ownb"), own)
+        mm(V2("b4", 24, 32), IdM, V2("s256"), True, False)
+        mm(V2("b4", 24, 32), V2("Tri"), cnt, False, True)
+        mm(V2("b4", 16, 24), V2("Tri"), cnt, True, True)
+        tt(V2("Dc"), V2("Pc"), V2("b2"), A.mult)
+        for s in range(N):
+            mm(f2, IdM, V2("Dc", 64 * s, 64 * s + 64), s == 0, False)
+        for s in range(N):
+            ts(V2("Of", 64 * s, 64 * s + 64), V2("ownb"), float(owner[s]), V2("b4", 24 + s, 25 + s), A.is_equal, A.mult)
+            mm(f2, V2("I1"), V2("Of", 64 * s, 64 * s + 64), False, s == N - 1)
+        fill(V3("rnS", 0, N, 0, 2), 0.0)
+        cp((T.rnS[:, :, 0], V3("rnS", 0, N, 0, 1)[1], N), V2("b4", 16, 24))
+        send([(s, owner[s], V3("rnS", s, s + 1, 0, 2), T.rn[:, s, :]) for s in FAR], "rn")
+        ts(V2("fh"), f2, 0.0625, -8.5 / 16, A.mult, A.add)
+        ts(V2("fa"), f2, 128.0, -128.0, A.mult, A.add)
+        ts(V2("b6", 0, 64), V2("fh"), -2047.0, None, A.mult)
+        tt(V2("Zk"), V2("fa"), V2("b6", 0, 64), A.add)
+        cp(V2("F2u"), V2("Zk"))
+
+    def cands():
+        ts(V2("loC"), V2("loI"), -2048.0, None, A.add)
+        ts(V2("hiC"), V2("hiI"), -2048.0, None, A.add)
+        w = 256 // PARTS
+        ts(V2("Rlo", 0, w), V2("uC", 0, w), V2("pmF"), V2("loC"), A.is_equal, A.mult)
+        mm(V2("b0", 0, w), V2("G1"), V2("Rlo", 0, w), True, True)
+        ts(V2("Rhi", 0, w), V2("uC", 0, w), V2("pmF"), V2("hiC"), A.is_equal, A.mult)
+        mm(V2("b7", 0, w), V2("Gc"), V2("oneb", 0, w), True, False)
+        mm(V2("b7", 0, w), V2("G64"), V2("Rhi", 0, w), False, True)
+        act(V2("nC"), V2("iotaC"), F.Identity, bias=V2("cxF"))
+        for a in range(0, 256, w):
+            def H(nm, o=0):
+                return V2(nm, o + a, o + a + w)
+            tt(H("hx"), H("nC"), V2("b0", 0, w), A.add)
+            ts(H("hL"), H("hx"), 4095, None, A.bitwise_and)
+            cp(H("Lf"), H("hL"))
+            act(H("hq"), H("Lf"), F.Square)
+            act(H("b1"), H("Lf"), F.Identity, scale=64.0, bias=-262144.0)
+            tt(H("ht"), H("hq"), V2("b7", 0, w), A.add)
+            ts(H("hB"), H("ht"), 6, 4095, A.arith_shift_right, A.bitwise_and)
+            cp(H("Bf"), H("hB"))
+            act(H("hb"), H("Bf"), F.Square)
+            act(H("b7", 256), H("Bf"), F.Identity, scale=4096.0, bias=2048.0)
+            tt(H("hu"), H("hb"), H("b1"), A.add)
+            ts(H("he"), H("hu"), 7, 2047, A.arith_shift_right, A.bitwise_and)
+            cp(H("hv"), H("he"))
+            tt(H("hv", 256), H("he"), H("b7", 256), A.add)
+            for o in (0, 4):
+                for v in range(o + a // 64, o + (a + w) // 64):
+                    dma("ys"[v % 2], row("VxS", v), V2("hv", 64 * v, 64 * v + 64), [("VxS", 0, 1024)])
+
+    def scatter():
+        iota(V2("jc"), [[16, LC], [0, 3], [1, 16]], 0, 0, True, [V3("rnS", 0, N, 0, 1)])
+        iota(V2("p4"), [[1, 128]], 0, 0, True)
+        aff(V2("Za"), V2("Zs"), [[-16, 9], [0, 16]], A.is_ge, 0, 1)
+        aff(V2("Zt"), V2("Za"), [[16, 9], [0, 16]], A.is_ge, 2, -1)
+        aff(V2("Zs"), V2("Za"), [[16, 9], [0, 16]], A.is_ge, 15, -1)
+        fill(E("sI", 0, N, 0, 1), 0)
+        aff(V2("Zi"), V2("Zs"), [[-16, 9], [0, 16]], A.is_ge, -3, 1)
+        aff(V2("Zi"), V2("Zi"), [[16, 9], [0, 16]], A.is_ge, 4, -1)
+        cp(IX(V2("Vwin"), V2("F2u")), rows("VxS"))
+        for nm in ("land", "IDx"):
+            for s in range(N):
+                act(V2(nm, SW * s + CAPQ, SW * s + SW), V2("rst", 0, SW - CAPQ), scale=0.0)
+        for v in range(8):
+            dma("ys"[v % 2], V3("fv%d" % v, 0, N, 0, 16), (T.Vwin[v:128:16, :], [("Vwin", 0, 2048)], 128))
+
+    def lists():
+        for nm, f, v in (("le", cp, 0), ("msg", act, 4)):
+            for i in range(4):
+                f((T[nm][:, :, 3 - i:48:4], [(nm, 48 * s + 3 - i, 48 * s + 4 - i) for s in range(N)], N * LC), V3("fv%d" % (v + i), 0, N, 0, LC))
+        act(V3("rq", S0, S0 + 1, 0, 48), V3("msg", S0, S0 + 1, 0, 48))
+        for gr in GRP:
+            send([(s, owner[s], V3("le", s, s + 1, 0, 48), T.rl[:, 48 * s:48 * s + 48]) for s in gr], "rl")
+        for gr in GRP:
+            send([(s, owner[s], V3("msg", s, s + 1, 0, 48), T.rq[:, s, :]) for s in gr], "rq")
 
     def piece(j):
-        dma("y", (T.W1[j:128:16, :], [("W1p%d" % j, 0, 2048)]), V2("p%d" % j), [("W1", 0, 2048)])
+        dma("y", row("W1", j), V2("p%d" % j), [("W1", 0, 2048)])
 
     def pieces():
         piece(4)
         ts(V2("T0"), V2("thrI"), 4096.0, None, A.mult)
         tt(V2("T1"), V2("T0"), V2("aliI"), A.add)
-        ts(V2("T2"), V2("T1"), 16777216.0, None, A.min)
-        cp(V2("p0"), V2("T2"))
-        tt(V2("r1"), V2("T2"), V2("p0"), A.subtract)
-        cp(V2("p1"), V2("r1"))
-        tt(V2("p2"), V2("r1"), V2("p1"), A.subtract)
+        cp(V2("p0"), V2("T1"))
+        tt(V2("T0"), V2("T1"), V2("p0"), A.subtract)
+        cp(V2("p1"), V2("T0"))
+        tt(V2("p2"), V2("T0"), V2("p1"), A.subtract)
         for j in range(3):
             piece(j)
-    tab = (T.W1[:], [("W1", 0, 2048)] + [("W1p%d" % j, 0, 2048) for j in (0, 1, 2, 4)])
+    tab = rows("W1")
 
-    def RN(s, k):
-        return V3("rnS" if s == S0 else "rn", s, s + 1, k, k + 1)
-
-    for s in range(N):
-        act(V2("ab", CAPQ * s, CAPQ * s + CAPQ), V2("jc"), F.Abs, bias=RN(s, 0))
-
-    def masks(a, b):
-        for s in range(a, b):
-            ts(V2("mk", CAPQ * s, CAPQ * s + CAPQ), V2("ab", CAPQ * s, CAPQ * s + CAPQ), RN(s, 1), float(2 ** (20 - asker[s])), A.is_lt, A.mult)
+    def masks():
+        op("g", lambda: g.affine_select(T.Md[:], T.Id[:], [[1, 128]], A.not_equal, -1.0, -1, -1), [V2("Md")], [IdM])
+        tt(V2("Md"), V2("Md"), V2("BD"), A.mult)
+        for z in range(4):
+            mm(V2(TB[z % 2]), V2("Md"), V2("seenS", 512 * z, 512 * z + 512), True, True)
+            act(V2("seenD", 512 * z, 512 * z + 512), V2(TB[z % 2]))
+        for s in range(N):
+            ts(V2("mk", 576 * s, 576 * s + 576), V2("jc"), V3("rnS" if s == S0 else "rn", s, s + 1, 0, 1), float(2 ** (20 - asker[s])), A.is_ge, A.mult)
 
     def ylist():
-        ts(V2("F2i"), f2, -1.0, None, A.add)
-        ts(V2("own176"), V2("ownb"), 176.0, None, A.mult)
+        ts(V2("yo"), f2, -1.0, None, A.add)
         ts(V2("own2k"), V2("ownb"), 2048.0, None, A.mult)
-        ts(V2("ya"), V2("F2i"), 10923.0, None, A.mult)
-        ts(V2("yc"), V2("F2i"), 16.0, None, A.mult)
-        ts(V2("yb"), V2("ya"), 17, None, A.arith_shift_right)
-        tt(V2("yc"), V2("yc"), V2("own176"), A.add)
-        ts(V2("yb"), V2("yb"), -191.0, None, A.mult)
-        tt(V2("yd"), V2("yb"), V2("yc"), A.add)
-        cp(V2("yo"), V2("yd"))
-
-    def hashes(c):
-        a, b = HS[c]
-
-        def W(nm):
-            return V3(nm, a, b, 0, 48)
-
-        def out(sem, src, dst):
-            for gr in GRP:
-                if a <= gr[0] < b:
-                    send([(s, owner[s], src(s), dst(s)) for s in gr], sem)
-        e = b if c == 0 else N
-        for i in range(4 if c < 2 else 0):
-            kk = ((1597 * (i + 1)) & 4095) - 4096
-            ts(V3("hx", a, e, LC * i, LC * i + LC), V3("vl", a, e, 0, LC), 4096.0 * kk + 2048.0 * 4097.0, None, A.add)
-        ts(W("hL"), W("hx"), 12, 4095, A.arith_shift_right, A.bitwise_and)
-        ts(W("h4"), W("hx"), 4095, None, A.bitwise_and)
-        tt(W("hq"), W("hL"), W("hL"), A.mult)
-        p = V2("b6", 48 * a, 48 * b)
-        ts(p, W("h4"), 64.0, -262144.0, A.mult, A.add)
-        tt(W("ht"), W("hq"), p, A.add)
-        ts(p, W("hL"), 64.0, -262144.0, A.mult, A.add)
-        ts(W("hB"), W("ht"), 6, 4095, A.arith_shift_right, A.bitwise_and)
-        tt(W("hb"), W("hB"), W("hB"), A.mult)
-        tt(W("hu"), W("hb"), p, A.add)
-        ts(p, W("hB"), 4096.0, 2048.0, A.mult, A.add)
-        ts(W("he"), W("hu"), 7, 2047, A.arith_shift_right, A.bitwise_and)
-        cp(V2("le", 48 * a, 48 * b), W("he"))
-        out("rl", lambda s: V2("le", 48 * s, 48 * s + 48), lambda s: T.rl[:, 48 * s:48 * s + 48])
-        tt(W("msg"), W("he"), p, A.add)
-        out("rq", lambda s: V3("msg", s, s + 1, 0, 48), lambda s: T.rq[:, s, :])
 
     def look(c):
         a, b = CH[c]
-        lst = "le" if a == S0 else "rl"
         for s in range(a, b):
-            act(V2("GT", 768 * s, 768 * s + 768), IX(tab, V2(lst, 48 * s, 48 * s + 48)))
+            lst = V3("le", s, s + 1, 0, 48) if s == S0 else V2("rl", 48 * s, 48 * s + 48)
+            (cp if s in GV else act)(V2("GT", 768 * s, 768 * s + 768), IX(tab, lst))
 
     def arrive(c):
         a, b = CH[c]
-        for i in range(16):
-            mm(V2(TB[c % 3], 0, 48 * (b - a)), Z("Zt", i), V2("GT", 768 * a + i, 768 * b, 16), i == 0, i == 15)
+        back(V2(TB[c % 3], 0, 48 * (b - a)), "Zt", "GT", 768 * a, 768 * b)
 
     def filt(c):
         a, b = CH[c]
-        tt(V3("mn", a, b, 0, 48), V3("msg" if a == S0 else "rq", a, b, 0, 48), V2(TB[c % 3], 0, 48 * (b - a)), A.min)
-        ts(V3("cI", a, b, 0, 48), V3("mn", a, b, 0, 48), 2047, None, A.bitwise_and)
-        cp(V2("ls", 36 * a, 36 * b), V3("cI", a, b, 0, 36))
-        for s in range(a, b):
-            for i in range(3):
-                o = 576 * s + CAPQ * i
-                tt(V2("MG", o, o + CAPQ), IX(V2("seenS"), V2("ls", 36 * s + LC * i, 36 * s + LC * i + LC)), V2("mk", CAPQ * s, CAPQ * s + CAPQ), A.mult)
-        o = V2("b%d" % (2 + c % 2), 0, 36 * (b - a))
-        mm(o, IdM, V2("Ci", 0, 36 * (b - a)), True, False)
-        for i in range(16):
-            mm(o, Z("Zs", i), V2("MG", 576 * a + i, 576 * b, 16), False, i == 15)
-        ts(V3("ky", a, b, 36, 48), V3("cI", a, b, 36, 48), 6144.0, None, A.add)
+        tt(V3("mn", a, b, 0, 48), V3("rq", a, b, 0, 48), V2(TB[c % 3], 0, 48 * (b - a)), A.min)
+        ts(E("cI", a, b, 0, 4), V3("mn", a, b, 0, 48), 2047, None, A.bitwise_and)
+        cp(V2("ls", 36 * a, 36 * b), E("cI", a, b, 1, 4))
+        for o in range(36 * a, 36 * b, MGW):
+            tt(V2("MG", 16 * o, 16 * (o + MGW)), IX(V2("seenD"), V2("ls", o, o + MGW)), V2("mk", 16 * o, 16 * (o + MGW)), A.mult)
+            due[len(calls) - 1] = DUE[c][0]
+        back(V2("b%d" % (2 + c % 2), 0, 36 * (b - a)), "Zs", "MG", 576 * a, 576 * b)
 
     def pick(c):
         a, b = CH[c]
-        cp(V2("sI", 36 * a, 36 * b), V2("b%d" % (2 + c % 2), 0, 36 * (b - a)))
-        ts(V3("sb", a, b, 0, 36), V2("sI", 36 * a, 36 * b), 2 ** 20 + 3 * 2048, None, A.bitwise_and)
-        tt(V3("ky", a, b, 0, 36), V3("sb", a, b, 0, 36), V3("cI", a, b, 0, 36), A.add)
-        tt(V3("m2", a, b, 0, 24), V3("ky", a, b, 0, 24), V3("ky", a, b, 24, 48), A.min)
-        x = (LC * a, LC * b)
-        tt(V2("kc", *x), V3("m2", a, b, 0, 12), V3("m2", a, b, 12, 24), A.min)
-        ts(V2("xI", *x), V2("kc", *x), 2047, None, A.bitwise_and)
-        cp(V2("lx", *x), V2("xI", *x))
-        if a == S0:
-            act(V2("land", CAPQ * me, CAPQ * me + CAPQ), IX(V2("vecS"), V2("lx", *x)))
-            return
-        act(V2("rs", CAPQ * a, CAPQ * b), IX(V2("vecS"), V2("lx", *x)))
+        w, x = (48 * a, 48 * b), (LC * a, LC * b)
+        cp(E("sI", a, b, 1, 4), V2("b%d" % (2 + c % 2), 0, 36 * (b - a)))
+        ts(V2("sb", *w), E("sI", a, b, 0, 4), 2 ** 20, None, A.bitwise_and)
+        tt(V2("kb", *w), E("cI", a, b, 0, 4), V2("sb", *w), A.subtract)
+        cp(V2("ka", *w), V2("sb", *w))
+        scan(V2("kc", *w), V2("ka", *w), V2("kb", *w), A.min, A.max)
+        cp(V2("lx", *x), V2("kc", 48 * a + 3, 48 * b, 4))
+        due[len(calls) - 1] = DUE[c][1]
+        far = [s for s in range(a, b) if s != S0]
+        if far:
+            act(V2("rs", CAPQ * far[0], CAPQ * far[-1] + CAPQ), IX(V2("vecS"), V2("lx", LC * far[0], LC * far[-1] + LC)))
+        if a <= S0 < b:
+            act(V2("land", SW * S0, SW * S0 + CAPQ), IX(V2("vecS"), V2("lx", LC * S0, LC * S0 + LC)))
         for gr in GRP:
             if a <= gr[0] < b:
                 send([(s, asker[s], V2("lx", LC * s, LC * s + LC), T.lr[:, LC * s:LC * s + LC]) for s in gr], "lr")
-                send([(s, asker[s], V2("rs", CAPQ * s, CAPQ * s + CAPQ), T.land[:, CAPQ * me:CAPQ * me + CAPQ]) for s in gr], "la")
+                send([(s, asker[s], V2("rs", CAPQ * s, CAPQ * s + CAPQ), T.land[:, SW * s:SW * s + CAPQ]) for s in gr], "la")
 
     def items(c):
         for s in range(*CH[c]):
-            o = CAPQ * owner[s]
-            act(V2("IDx", o, o + CAPQ), IX(tab, V2("lx" if s == S0 else "lr", LC * s, LC * s + LC)))
+            act(V2("IDx", SW * s, SW * s + CAPQ), IX(tab, V2("lx" if s == S0 else "lr", LC * s, LC * s + LC)))
 
-    BLOCK = {"H": hashes, "G": look, "A": arrive, "F": filt, "P": pick, "I": items, "Y": ylist, "M": masks, "T": pieces}
-    for blocks in PLAN:
-        turns = []
-        for n, (k, f, *y) in enumerate(blocks):
-            stream[0] = []
-            BLOCK[f](*y)
-            started = False
-            for (q, h) in stream[0]:
-                k += 1 if q == "v" and started else 0
-                started = True
-                turns.append((k, n, len(turns), h))
-        stream[0] = None
-        for x in sorted(turns, key=lambda x: x[:3]):
-            x[3]()
+    for f in (owners, cands, scatter, pieces, ylist, lists):
+        f()
+    masks()
+    for c in ORDER:
+        for f in (look, arrive, filt, pick, items):
+            f(c)
 
     def ygat(h):
         return V2("yS", 512 * h, 512 * h + 512), IX(V2("land"), V2("yo", 32 * h, 32 * h + 32))
@@ -465,11 +552,11 @@ def rank_program(g, core, T, topo):
     cp(*ygat(0))
     dma("y", hbm(T.y[:, 0:512]), V2("yS", 0, 512))
     act(*ygat(1))
-    for i in range(16):
-        mm(V2("b4", 64, 128), Z("Zi", i), V2("IDg", i, 1024, 16), i == 0, i == 15)
+    back(V2("b4", 64, 128), "Zi", "IDg", 0, 1024)
     tt(V2("chS"), V2("own2k"), V2("b4", 64, 128), A.add)
     dma("s", hbm(T.y[:, 512:1024]), V2("yS", 512, 1024))
     dma("s", hbm(T.chosen[:]), V2("chS"))
+    issue()
 
     for s, n in count.items():
         if clock["g"].get(s, 0) < n:

@@ -4,19 +4,27 @@ from concourse.mybir import AluOpType, ActivationFunctionType
 A = AluOpType
 F = ActivationFunctionType
 N = 8
-CAPQ, LC, SW = 192, 12, 256
+CAPQ, LC, SW = 192, 12, 192
 S0 = 7
 CH = [(0, 2), (2, 4), (4, 6), (6, 7), (7, 8)]
 GRP = [(0, 1), (2, 3), (4, 5), (6,)]
 ORDER = [4, 0, 1, 2, 3]
 DUE = [(16.2, 13.7), (14.1, 11.5), (11.8, 9.4), (10.7, 8.5), (18.4, 8.0)]
-COST = {"cycle": 0.0009, "gather": 0.0013, "scatter": 0.0025, "mm": 0.0007, "wait": 0.2, "dma": 0.06, "load": 1.3, "byte": 0.0005, "call": 0.4, "far": 1.8, "first": 2.0, "link": 1.0}
+COST = {"cycle": 0.00085, "gather": 0.0013, "scatter": 0.0031, "mm": 0.0006, "wait": 0.23, "dma": 0.08, "load": 1.1, "byte": 0.0004, "call": 0.35, "far": 1.3, "first": 1.8, "link": 1.0}
 AHEAD, TURNS = 0.2, 1
-SOON = {"rn": 6.0, "W1": 3.0}
-MGW = 36
-PARTS = 2
+SOON = {"rn": 5.0, "W1": 3.0, "VxS": 0.8}
+MGW = [36, 36, 36, 36, 36]
+PARTS = 4
 ROW = 1 << 16
-GV = (1,)
+GV = {1: 48, 7: 24}
+IV = (2, 4, 6)
+IL = (2, 3, 4, 5, 6)
+SENDS = [("rl", 0), ("rl", 1), ("rq", 0), ("rl", 2), ("rq", 1), ("rl", 3), ("rq", 2), ("rq", 3)]
+YP = 4
+LT = 2
+SHORT = 2.0
+MK = (7, 0, 1, 2, 3)
+PB = "b5"
 TB = ["b0", "b1", "b7"]
 f32, b16, i32, u16, f16 = "float32", "bfloat16", "int32", "uint16", "float16"
 SHAPES = {
@@ -24,19 +32,17 @@ SHAPES = {
           "loI": 1, "hiI": 1, "Lr": 64, "Lq": 64, "t1": 64, "Bq": 64, "Lp": 64, "t2": 64, "w12": 64, "fh": 64,
           "hx": 256, "hL": 256, "ht": 256, "hB": 256, "hu": 256, "he": 256,
           "mn": (8, 48), "cI": (96, 4), "sI": (96, 4), "sb": 384},
-    f32: {"rkF": 16, "BDf": 128, "w1c": 8, "w4c": 8, "sdF": 1, "pgF": 1, "iotaC": 256, "hpF": 1, "Zk": 64, "tA": 8, "dA": 8, "dB": 8,
-          "pmF": 1, "cxF": 1, "nC": 256, "loC": 1, "hiC": 1, "hv": 512, "fa": 64, "Lf": 256, "Bf": 256, "hq": 256, "hb": 256,
-          "VxS": 1024, "Vwin": 2048, "own2k": 64, "T0": 128, "T1": 128,
+    f32: {"rkF": 16, "BDf": 128, "w1c": 8, "w4c": 8, "sdF": 1, "pgF": 1, "iotaC": 256, "hpF": 1, "Zk": 64, "tA": 8, "dA": 8, "dB": 8, "dH": 8,
+          "pmF": 1, "cxF": 1, "nC": 256, "loC": 1, "hiC": 1, "hv": 256, "fa": 64, "Lf": 256, "Bf": 256, "hq": 256, "hb": 256,
+          "VxS": 1024, "Vwin": 1536, "fv": 384, "own2k": 64, "T0": 128, "T1": 128,
           "msg": (8, 48), "rq": (8, 48), "chS": 64, "ka": 384, "kb": 384, "kc": 384},
     b16: {"seenS": 2048, "vecS": 2048, "W1": 2048, "oneb": 256, "gC": 128, "Gc": 128, "Id": 128, "Tri": 128, "BD": 128, "rst": 512, "uC": 256, "s256": 8,
-          "Zs": 144, "Za": 144, "Zt": 144, "Zi": 144, "jc": 576, "stp": 1024, "Pc": 512, "Dc": 512, "ownb": 64,
-          "p0": 128, "p1": 128, "p2": 128, "p4": 128, "rs": 1536, "land": 2048, "seenD": 2048, "Md": 128, "rnS": (8, 2), "rn": (8, 2), "mk": 4608, "GT": 6144, "MG": 4608,
-          "IDx": 2048, "IDg": 1024, "yS": 1024},
+          "Zs": 144, "Za": 144, "Zt": 144, "Zi": 144, "jc": 576, "stp": 1024, "Dg": 1024, "Pc": 512, "Dc": 512, "ownb": 64,
+          "p0": 128, "p1": 128, "p2": 128, "p4": 128, "rs": 1536, "land": 1536, "seenD": 2048, "Md": 128, "rnS": (8, 2), "rn": (8, 2), "mk": 4608, "GT": 6144, "MG": 4608,
+          "IDx": 1536, "IDg": 1024, "yS": 1024},
     u16: {"F2u": 64, "yo": 64, "le": (8, 48), "rl": 384, "lx": 96, "lr": 96, "ls": 288},
     f16: {"I1": 128, "G1": 128, "G64": 128, "Rlo": 256, "Rhi": 256, "Of": 512},
 }
-for _v in range(8):
-    SHAPES[f32]["fv%d" % _v] = (8, 16)
 SCRATCH = {}
 for _dt, _d in SHAPES.items():
     for _k, _n in _d.items():
@@ -116,7 +122,7 @@ def rank_program(g, core, T, topo):
                 log.setdefault(k, []).append((lo, hi, w, tok, q))
 
     calls = []
-    moved, soon, due, LINK = {}, {}, {}, ("link", 0, 1)
+    moved, soon, due, long, LINK = {}, {}, {}, set(), ("link", 0, 1)
 
     def regs(views):
         return [r for x in views for r in x[1]]
@@ -160,7 +166,9 @@ def rank_program(g, core, T, topo):
 
         def gap(i, j, early=0):
             if LINK in calls[i][3] and LINK in calls[j][3]:
-                return COST["link"]
+                return COST["link"] * (calls[i][3][0][0] == "land")
+            if ("turn", 0, 1) in calls[i][3] and ("turn", 0, 1) in calls[j][3]:
+                return 0.0
             return 0.0 if calls[i][0] == calls[j][0] == "t" else calls[i][5] + moved.get(i, 0.0) + early * soon.get(i, 0.0)
         banks = [{k for (k, lo, hi) in c[2] + c[3] if k in BANKS} for c in calls]
 
@@ -172,7 +180,7 @@ def rank_program(g, core, T, topo):
             while ready:
                 st = {j: max([ready[j], free[calls[j][0]]] + [bank[k][1] for k in banks[j] if k in bank and bank[k][0] != calls[j][0]]) for j in ready}
                 first = min(ready, key=lambda j: (st[j], -way[j], j))
-                j = min((i for i in ready if calls[i][0] == calls[first][0] and st[i] <= st[first] + min(AHEAD * calls[first][4], 0.5)), key=lambda i: (-way[i], i))
+                j = min((i for i in ready if calls[i][0] == calls[first][0] and st[i] <= st[first] + min(AHEAD * calls[first][4], 0.5)), key=lambda i: (SHORT * (i in long) - way[i], i))
                 q = calls[j][0]
                 order.append(j)
                 free[q] = end[j] = st[j] + calls[j][4]
@@ -285,7 +293,7 @@ def rank_program(g, core, T, topo):
         size = len(pairs) * pairs[0][2][2] * (4 if wide(pairs[0][2]) else 2)
         moved[len(calls)] = 2 * COST["byte"] * size
         soon[len(calls)] = SOON.get(sem, 0.0)
-        calls.append(("g", lambda: send_now(pairs, sem), regs([x[2] for x in pairs]), regs([LAND[sem](x[0]) for x in pairs]) + [LINK] * (sem == "la"),
+        calls.append(("g", lambda: send_now(pairs, sem), regs([x[2] for x in pairs]), regs([LAND[sem](x[0]) for x in pairs]) + [LINK] * (sem in ("lr", "la")),
                       COST["call"] + (COST["first"] if sem == "rn" else 0), COST["far"]))
 
     def hops(d):
@@ -318,7 +326,6 @@ def rank_program(g, core, T, topo):
     dma("y", V2("thrI"), hbm(T.thr[:]), V2("sdI")[1])
     dma("y", V2("aliI"), hbm(T.ali[:]), V2("sdI")[1])
     dma("y", V2("seenS"), hbm(T.seen[:]), V2("rkI")[1])
-    dma("y", V2("vecS"), hbm(T.vec[:]), V2("rkI")[1])
 
     fill(V2("oneb"), 1.0)
     fill(V2("rst"), 1.0)
@@ -343,9 +350,8 @@ def rank_program(g, core, T, topo):
     cp(V2("pmF"), V2("pm"))
     ts(V2("cxF"), V2("pm"), 4.0 * 7985.0, None, A.mult)
 
-    for nm, n in (("VxS", 2), ("Vwin", 4)):
-        for z in range(n):
-            act(V2(nm, 512 * z, 512 * z + 512), V2("rst"), scale=0.0)
+    for z in range(2):
+        act(V2("VxS", 512 * z, 512 * z + 512), V2("rst"), scale=0.0)
     ts(V2("loI"), V2("sdI"), 4095, None, A.bitwise_and)
     ts(V2("hiI"), V2("sdI"), 12, None, A.arith_shift_right)
 
@@ -375,22 +381,23 @@ def rank_program(g, core, T, topo):
         act(V2("s256"), V2("w1c"), scale=float(SW))
         tt(V2("Zk"), V2("w12"), V2("Bq"), A.add)
         cp(V2("I1"), V2("Id"))
-        k = 0
+        op("s", lambda: g.scalar.activation(T.dH[:, 0:7], T.dB[:, 0:7], F.Copy, scale=0.5, accum_out=T.dH[:, 7:8]), [V2("dH")], [V2("dB")])
         for w in range(8):
-            ts(V2("stp", 64 * k, 64 * k + 64), V2("Zk"), V2("tA", w, w + 1), V2("dA", w, w + 1), A.is_ge, A.mult)
-            mm(own, IdM, V2("stp", 64 * k, 64 * k + 64), k == 0, k == 14)
-            k += 1
+            act(V2("Dg", 128 * w, 128 * w + 128), IdM, scale=V2("dH", w, w + 1))
+        mm(own, V2("Dg", 896, 1024), V2("oneb", 0, 64), True, False)
+        for w in range(8):
+            ts(V2("stp", 128 * w, 128 * w + 64), V2("Zk"), V2("tA", w, w + 1), V2("dA", w, w + 1), A.is_ge, A.mult)
+            mm(own, IdM, V2("stp", 128 * w, 128 * w + 64), False, w == 7)
             if w < 7:
-                ts(V2("stp", 64 * k, 64 * k + 64), V2("Zk"), 4096.0 * (w + 1), V2("dB", w, w + 1), A.is_ge, A.mult)
-                mm(own, IdM, V2("stp", 64 * k, 64 * k + 64), False, False)
-                k += 1
+                act(V2("stp", 128 * w + 64, 128 * w + 128), V2("Zk"), F.Sign, bias=0.5 - 4096.0 * (w + 1))
+                mm(own, V2("Dg", 128 * w, 128 * w + 128), V2("stp", 128 * w + 64, 128 * w + 128), False, False)
         for s in range(N):
             ts(V2("b2", 64 * s, 64 * s + 64), own, float(owner[s]), None, A.is_equal)
         scan(V2("Pc"), V2("rst"), V2("b2"), A.mult, A.add)
-        cp(V2("ownb"), own)
+        act(V2("ownb"), own)
         mm(V2("b4", 24, 32), IdM, V2("s256"), True, False)
         mm(V2("b4", 24, 32), V2("Tri"), cnt, False, True)
-        mm(V2("b4", 16, 24), V2("Tri"), cnt, True, True)
+        mm(V2("b1", 256, 264), V2("Tri"), cnt, True, True)
         tt(V2("Dc"), V2("Pc"), V2("b2"), A.mult)
         for s in range(N):
             mm(f2, IdM, V2("Dc", 64 * s, 64 * s + 64), s == 0, False)
@@ -398,13 +405,11 @@ def rank_program(g, core, T, topo):
             ts(V2("Of", 64 * s, 64 * s + 64), V2("ownb"), float(owner[s]), V2("b4", 24 + s, 25 + s), A.is_equal, A.mult)
             mm(f2, V2("I1"), V2("Of", 64 * s, 64 * s + 64), False, s == N - 1)
         fill(V3("rnS", 0, N, 0, 2), 0.0)
-        cp((T.rnS[:, :, 0], V3("rnS", 0, N, 0, 1)[1], N), V2("b4", 16, 24))
-        send([(s, owner[s], V3("rnS", s, s + 1, 0, 2), T.rn[:, s, :]) for s in FAR], "rn")
+        act((T.rnS[:, :, 0], V3("rnS", 0, N, 0, 1)[1], N), V2("b1", 256, 264))
         ts(V2("fh"), f2, 0.0625, -8.5 / 16, A.mult, A.add)
-        ts(V2("fa"), f2, 128.0, -128.0, A.mult, A.add)
-        ts(V2("b6", 0, 64), V2("fh"), -2047.0, None, A.mult)
-        tt(V2("Zk"), V2("fa"), V2("b6", 0, 64), A.add)
-        cp(V2("F2u"), V2("Zk"))
+        ts(V2("fa"), f2, 96.0, -96.0, A.mult, A.add)
+        ts(V2("b6", 0, 64), V2("fh"), -1535.0, None, A.mult)
+        tt(V2("F2u"), V2("fa"), V2("b6", 0, 64), A.add)
 
     def cands():
         ts(V2("loC"), V2("loI"), -2048.0, None, A.add)
@@ -428,14 +433,12 @@ def rank_program(g, core, T, topo):
             ts(H("hB"), H("ht"), 6, 4095, A.arith_shift_right, A.bitwise_and)
             cp(H("Bf"), H("hB"))
             act(H("hb"), H("Bf"), F.Square)
-            act(H("b7", 256), H("Bf"), F.Identity, scale=4096.0, bias=2048.0)
+            act(H("b7", 256), H("Bf"), scale=4096.0)
             tt(H("hu"), H("hb"), H("b1"), A.add)
             ts(H("he"), H("hu"), 7, 2047, A.arith_shift_right, A.bitwise_and)
-            cp(H("hv"), H("he"))
-            tt(H("hv", 256), H("he"), H("b7", 256), A.add)
-            for o in (0, 4):
-                for v in range(o + a // 64, o + (a + w) // 64):
-                    dma("ys"[v % 2], row("VxS", v), V2("hv", 64 * v, 64 * v + 64), [("VxS", 0, 1024)])
+            tt(H("hv"), H("he"), H("b7", 256), A.add)
+            for v in range(a // 64, (a + w) // 64):
+                dma("y", row("VxS", v), V2("hv", 64 * v, 64 * v + 64), [("VxS", 0, 1024)])
 
     def scatter():
         iota(V2("jc"), [[16, LC], [0, 3], [1, 16]], 0, 0, True, [V3("rnS", 0, N, 0, 1)])
@@ -446,56 +449,69 @@ def rank_program(g, core, T, topo):
         fill(E("sI", 0, N, 0, 1), 0)
         aff(V2("Zi"), V2("Zs"), [[-16, 9], [0, 16]], A.is_ge, -3, 1)
         aff(V2("Zi"), V2("Zi"), [[16, 9], [0, 16]], A.is_ge, 4, -1)
+        send([(s, owner[s], (T.rnS[:, s, :], V3("rnS", s, s + 1, 0, 2)[1] + V2("hv")[1], 2), T.rn[:, s, :]) for s in FAR], "rn")
+        for z in range(3):
+            act(V2("Vwin", 512 * z, 512 * z + 512), V2("rst"), scale=0.0)
+            calls[-1][2].extend(V2("hb")[1])
         cp(IX(V2("Vwin"), V2("F2u")), rows("VxS"))
-        for nm in ("land", "IDx"):
-            for s in range(N):
-                act(V2(nm, SW * s + CAPQ, SW * s + SW), V2("rst", 0, SW - CAPQ), scale=0.0)
-        for v in range(8):
-            dma("ys"[v % 2], V3("fv%d" % v, 0, N, 0, 16), (T.Vwin[v:128:16, :], [("Vwin", 0, 2048)], 128))
+        for v in range(4):
+            dma("y", V2("fv", 96 * v, 96 * v + 96), (T.Vwin[v:128:16, :], V2("Vwin")[1], 96))
 
     def lists():
-        for nm, f, v in (("le", cp, 0), ("msg", act, 4)):
-            for i in range(4):
-                f((T[nm][:, :, 3 - i:48:4], [(nm, 48 * s + 3 - i, 48 * s + 4 - i) for s in range(N)], N * LC), V3("fv%d" % (v + i), 0, N, 0, LC))
+        for i in range(4):
+            ts(V2("b6", 96 * i, 96 * i + 96), V2("fv", 96 * i, 96 * i + 96), 1.5 * 2 ** 35, 1.5 * 2 ** 35, A.add, A.subtract)
+        for i in range(4):
+            le, msg = ((T[nm][:, :, 3 - i:48:4], [(nm, 48 * s + 3 - i, 48 * s + 4 - i) for s in range(N)], N * LC) for nm in ("le", "msg"))
+            y, r = V2("fv", 96 * i, 96 * i + 96), V2("b6", 96 * i, 96 * i + 96)
+            tt(le, y, r, A.subtract)
+            calls[-1][2].extend(V2("b6", 96 * LT, 96 * LT + 96)[1])
+            act(msg, y, F.Identity, bias=2048.0)
         act(V3("rq", S0, S0 + 1, 0, 48), V3("msg", S0, S0 + 1, 0, 48))
-        for gr in GRP:
-            send([(s, owner[s], V3("le", s, s + 1, 0, 48), T.rl[:, 48 * s:48 * s + 48]) for s in gr], "rl")
-        for gr in GRP:
-            send([(s, owner[s], V3("msg", s, s + 1, 0, 48), T.rq[:, s, :]) for s in gr], "rq")
+        for m, k in SENDS:
+            send([(s, owner[s], V3("le" if m == "rl" else "msg", s, s + 1, 0, 48), T.rl[:, 48 * s:48 * s + 48] if m == "rl" else T.rq[:, s, :]) for s in GRP[k]], m)
+            calls[-1][3].append(("turn", 0, 1))
+        dma("y", V2("vecS"), hbm(T.vec[:]), LAND["rl"](0)[1])
 
     def piece(j):
         dma("y", row("W1", j), V2("p%d" % j), [("W1", 0, 2048)])
 
     def pieces():
         piece(4)
-        ts(V2("T0"), V2("thrI"), 4096.0, None, A.mult)
-        tt(V2("T1"), V2("T0"), V2("aliI"), A.add)
-        cp(V2("p0"), V2("T1"))
-        tt(V2("T0"), V2("T1"), V2("p0"), A.subtract)
-        cp(V2("p1"), V2("T0"))
-        tt(V2("p2"), V2("T0"), V2("p1"), A.subtract)
+        t0, t1, t2 = (V2(PB, 128 * z, 128 * z + 128) for z in (1, 2, 3))
+        ts(t0, V2("thrI"), 4096.0, None, A.mult)
+        tt(t1, V2("aliI"), t0, A.add)
+        act(V2("p0"), t1)
+        tt(t2, t1, V2("p0"), A.subtract)
+        act(V2("p1"), t2)
+        tt(V2("p2"), t2, V2("p1"), A.subtract)
         for j in range(3):
             piece(j)
     tab = rows("W1")
 
     def masks():
-        op("g", lambda: g.affine_select(T.Md[:], T.Id[:], [[1, 128]], A.not_equal, -1.0, -1, -1), [V2("Md")], [IdM])
-        tt(V2("Md"), V2("Md"), V2("BD"), A.mult)
+        act(V2("Md"), V2("BD"), scale=-1.0)
+        aff(V2("Md"), V2("Md"), [[1, 128]], A.is_equal, -1, -1)
         for z in range(4):
-            mm(V2(TB[z % 2]), V2("Md"), V2("seenS", 512 * z, 512 * z + 512), True, True)
+            mm(V2(TB[z % 2]), IdM, V2("seenS", 512 * z, 512 * z + 512), True, False)
+            calls[-1][2].extend(V2("fh")[1])
+            mm(V2(TB[z % 2]), V2("Md"), V2("seenS", 512 * z, 512 * z + 512), False, True)
             act(V2("seenD", 512 * z, 512 * z + 512), V2(TB[z % 2]))
         for s in range(N):
             ts(V2("mk", 576 * s, 576 * s + 576), V2("jc"), V3("rnS" if s == S0 else "rn", s, s + 1, 0, 1), float(2 ** (20 - asker[s])), A.is_ge, A.mult)
+            calls[-1][2].extend(V2("Vwin")[1] if s in MK else V3("le", 0, N, 0, 48)[1])
 
     def ylist():
         ts(V2("yo"), f2, -1.0, None, A.add)
-        ts(V2("own2k"), V2("ownb"), 2048.0, None, A.mult)
+        calls[-1][2].extend(V2("Vwin")[1])
+        act(V2("own2k"), V2("ownb"), scale=2048.0)
 
     def look(c):
         a, b = CH[c]
         for s in range(a, b):
-            lst = V3("le", s, s + 1, 0, 48) if s == S0 else V2("rl", 48 * s, 48 * s + 48)
-            (cp if s in GV else act)(V2("GT", 768 * s, 768 * s + 768), IX(tab, lst))
+            for f, u, v in ((cp, 0, GV.get(s, 0)), (act, GV.get(s, 0), 48)):
+                if u < v:
+                    lst = (T.le[:, s, u:v], V3("le", s, s + 1, 0, 48)[1], v - u) if s == S0 else V2("rl", 48 * s + u, 48 * s + v)
+                    f(V2("GT", 768 * s + 16 * u, 768 * s + 16 * v), IX(tab, lst))
 
     def arrive(c):
         a, b = CH[c]
@@ -506,9 +522,11 @@ def rank_program(g, core, T, topo):
         tt(V3("mn", a, b, 0, 48), V3("rq", a, b, 0, 48), V2(TB[c % 3], 0, 48 * (b - a)), A.min)
         ts(E("cI", a, b, 0, 4), V3("mn", a, b, 0, 48), 2047, None, A.bitwise_and)
         cp(V2("ls", 36 * a, 36 * b), E("cI", a, b, 1, 4))
-        for o in range(36 * a, 36 * b, MGW):
-            tt(V2("MG", 16 * o, 16 * (o + MGW)), IX(V2("seenD"), V2("ls", o, o + MGW)), V2("mk", 16 * o, 16 * (o + MGW)), A.mult)
+        w = MGW[c]
+        for o in range(36 * a, 36 * b, w):
+            tt(V2("MG", 16 * o, 16 * (o + w)), IX(V2("seenD"), V2("ls", o, o + w)), V2("mk", 16 * o, 16 * (o + w)), A.mult)
             due[len(calls) - 1] = DUE[c][0]
+            long.add(len(calls) - 1)
         back(V2("b%d" % (2 + c % 2), 0, 36 * (b - a)), "Zs", "MG", 576 * a, 576 * b)
 
     def pick(c):
@@ -517,8 +535,7 @@ def rank_program(g, core, T, topo):
         cp(E("sI", a, b, 1, 4), V2("b%d" % (2 + c % 2), 0, 36 * (b - a)))
         ts(V2("sb", *w), E("sI", a, b, 0, 4), 2 ** 20, None, A.bitwise_and)
         tt(V2("kb", *w), E("cI", a, b, 0, 4), V2("sb", *w), A.subtract)
-        cp(V2("ka", *w), V2("sb", *w))
-        scan(V2("kc", *w), V2("ka", *w), V2("kb", *w), A.min, A.max)
+        scan(V2("kc", *w), V2("sb", *w), V2("kb", *w), A.min, A.max)
         cp(V2("lx", *x), V2("kc", 48 * a + 3, 48 * b, 4))
         due[len(calls) - 1] = DUE[c][1]
         far = [s for s in range(a, b) if s != S0]
@@ -533,29 +550,31 @@ def rank_program(g, core, T, topo):
 
     def items(c):
         for s in range(*CH[c]):
-            act(V2("IDx", SW * s, SW * s + CAPQ), IX(tab, V2("lx" if s == S0 else "lr", LC * s, LC * s + LC)))
+            (cp if s in IV else act)(V2("IDx", SW * s, SW * s + CAPQ), IX(tab, V2("lx" if s == S0 else "lr", LC * s, LC * s + LC)))
+            if s in IL:
+                held.append(calls[-1])
 
     for f in (owners, cands, scatter, pieces, ylist, lists):
         f()
     masks()
     for c in ORDER:
-        for f in (look, arrive, filt, pick, items):
+        for f in (look, arrive, filt, pick):
             f(c)
+    held = []
+    for c in ORDER:
+        items(c)
+    for x in held:
+        x[2].extend(V2("rs" if x[0] == "s" else "lx")[1])
 
-    def ygat(h):
-        return V2("yS", 512 * h, 512 * h + 512), IX(V2("land"), V2("yo", 32 * h, 32 * h + 32))
-
-    def igat(h):
-        return V2("IDg", 512 * h, 512 * h + 512), IX(V2("IDx"), V2("yo", 32 * h, 32 * h + 32))
-    act(*igat(1))
-    cp(*igat(0))
-    cp(*ygat(0))
-    dma("y", hbm(T.y[:, 0:512]), V2("yS", 0, 512))
-    act(*ygat(1))
+    for h in range(2):
+        (cp, act)[h](V2("IDg", 512 * h, 512 * h + 512), IX(V2("IDx"), V2("yo", 32 * h, 32 * h + 32)))
     back(V2("b4", 64, 128), "Zi", "IDg", 0, 1024)
     tt(V2("chS"), V2("own2k"), V2("b4", 64, 128), A.add)
-    dma("s", hbm(T.y[:, 512:1024]), V2("yS", 512, 1024))
-    dma("s", hbm(T.chosen[:]), V2("chS"))
+    dma("y", hbm(T.chosen[:]), V2("chS"))
+    w = 1024 // YP
+    for h in range(YP):
+        (cp, act)[h % 2](V2("yS", w * h, w * h + w), IX(V2("land"), V2("yo", w * h // 16, w * (h + 1) // 16)))
+        dma("ys"[h % 2], hbm(T.y[:, w * h:w * h + w]), V2("yS", w * h, w * h + w))
     issue()
 
     for s, n in count.items():

@@ -7,40 +7,54 @@ N = 8
 CAPQ, LC, SW = 192, 12, 192
 S0 = 7
 CH = [(0, 2), (2, 4), (4, 6), (6, 7), (7, 8)]
+PG = [(0, 2), (2, 4), (4, 6), (6, 8)]
 GRP = [(0, 1), (2, 3), (4, 5), (6,)]
-ORDER = [4, 0, 1, 2, 3]
-DUE = [(16.2, 13.7), (14.1, 11.5), (11.8, 9.4), (10.7, 8.5), (18.4, 8.0)]
-COST = {"cycle": 0.00085, "gather": 0.0013, "scatter": 0.0031, "mm": 0.0006, "wait": 0.23, "dma": 0.08, "load": 1.1, "byte": 0.0004, "call": 0.35, "far": 1.3, "first": 1.8, "link": 1.0}
+DUE = [16.2, 14.1, 11.8, 8.7, 11.0]
+DUP = [14.2, 11.5, 8.4, 8.5]
+DUT = [21.0, 17.0]
+EV = ()
+HW = 256
+RZ = 1
+MS = 1536
+HV = 2048
+HB = ["b0", "b1", "b2", "b3", "b7", "b4", "b0", "b1"]
+HO = [0, 1, 4, 5, 2, 3, 6, 7]
+COST = {"cycle": 0.00085, "gather": 0.0013, "scatter": 0.0031, "mm": 0.00059, "wait": 0.207, "dma": 0.08, "load": 0.98, "byte": 0.0004, "call": 0.35, "far": 1.43, "first": 1.8, "link": 1.0}
 AHEAD, TURNS = 0.2, 1
-SOON = {"rn": 5.0, "W1": 3.0, "VxS": 0.8}
-MGW = [36, 36, 36, 36, 36]
+SOON = {"rn": 4.5, "W1": 1.0, "VxS": 0.0}
+MGW = [36, 36, 18, 12, 12]
 PARTS = 4
 ROW = 1 << 16
-GV = {1: 48, 7: 24}
+GV = {7: 24}
 IV = (2, 4, 6)
 IL = (2, 3, 4, 5, 6)
 SENDS = [("rl", 0), ("rl", 1), ("rq", 0), ("rl", 2), ("rq", 1), ("rl", 3), ("rq", 2), ("rq", 3)]
+BACK = [("lr", 0), ("la", 0), ("lr", 1), ("la", 1), ("lr", 2), ("lr", 3), ("la", 2), ("la", 3)]
 YP = 4
 LT = 2
-SHORT = 2.0
-MK = (7, 0, 1, 2, 3)
+SC = 128
+GW = 24
+FQ = "yy"
+SHORT = 1.0
+MK = (0, 1, 2, 3)
 PB = "b5"
-TB = ["b0", "b1", "b7"]
+TB = ["b7", "b4", "b0", "b1", "b5"]
+FB = ["b2", "b3", "b2", "b3", "b6"]
 f32, b16, i32, u16, f16 = "float32", "bfloat16", "int32", "uint16", "float16"
 SHAPES = {
-    i32: {"sdI": 1, "rkI": 16, "thrI": 128, "aliI": 128, "iotaK": 64, "pI": 1, "pm": 1, "pg": 1,
+    i32: {"sdI": 1, "rkI": 16, "thrI": 128, "aliI": 128, "aliJ": 128, "iotaK": 64, "pI": 1, "pm": 1, "pg": 1,
           "loI": 1, "hiI": 1, "Lr": 64, "Lq": 64, "t1": 64, "Bq": 64, "Lp": 64, "t2": 64, "w12": 64, "fh": 64,
           "hx": 256, "hL": 256, "ht": 256, "hB": 256, "hu": 256, "he": 256,
           "mn": (8, 48), "cI": (96, 4), "sI": (96, 4), "sb": 384},
     f32: {"rkF": 16, "BDf": 128, "w1c": 8, "w4c": 8, "sdF": 1, "pgF": 1, "iotaC": 256, "hpF": 1, "Zk": 64, "tA": 8, "dA": 8, "dB": 8, "dH": 8,
           "pmF": 1, "cxF": 1, "nC": 256, "loC": 1, "hiC": 1, "hv": 256, "fa": 64, "Lf": 256, "Bf": 256, "hq": 256, "hb": 256,
-          "VxS": 1024, "Vwin": 1536, "fv": 384, "own2k": 64, "T0": 128, "T1": 128,
-          "msg": (8, 48), "rq": (8, 48), "chS": 64, "ka": 384, "kb": 384, "kc": 384},
+          "VxS": 1024, "Vwin": 1536, "fv": 384, "own2k": 64, "c0": 3, "fl": (8, 48), "fac": 288,
+          "msg": (8, 48), "rq": (8, 48), "chS": 64, "kb": 384, "kc": 384},
     b16: {"seenS": 2048, "vecS": 2048, "W1": 2048, "oneb": 256, "gC": 128, "Gc": 128, "Id": 128, "Tri": 128, "BD": 128, "rst": 512, "uC": 256, "s256": 8,
-          "Zs": 144, "Za": 144, "Zt": 144, "Zi": 144, "jc": 576, "stp": 1024, "Dg": 1024, "Pc": 512, "Dc": 512, "ownb": 64,
-          "p0": 128, "p1": 128, "p2": 128, "p4": 128, "rs": 1536, "land": 1536, "seenD": 2048, "Md": 128, "rnS": (8, 2), "rn": (8, 2), "mk": 4608, "GT": 6144, "MG": 4608,
+          "Zs": 144, "Za": 144, "Zt": 144, "Zi": 144, "jc": 576, "p3": 128, "Pc": 512, "Dc": 512, "ownb": 64,
+          "p0": 128, "p1": 128, "p2": 128, "p4": 128, "rs": 1536, "land": 1536, "seenD": 4096, "Md": 640, "hS": 2048, "sA": 2048, "hA": 2048, "rnS": (8, 2), "rn": (8, 2), "mk": 4608, "GT": 6144, "MG": 4608,
           "IDx": 1536, "IDg": 1024, "yS": 1024},
-    u16: {"F2u": 64, "yo": 64, "le": (8, 48), "rl": 384, "lx": 96, "lr": 96, "ls": 288},
+    u16: {"F2u": 64, "yo": 64, "le": (8, 48), "rl": 384, "lx": 96, "lr": 96, "aliU": 128},
     f16: {"I1": 128, "G1": 128, "G64": 128, "Rlo": 256, "Rhi": 256, "Of": 512},
 }
 SCRATCH = {}
@@ -122,7 +136,7 @@ def rank_program(g, core, T, topo):
                 log.setdefault(k, []).append((lo, hi, w, tok, q))
 
     calls = []
-    moved, soon, due, long, LINK = {}, {}, {}, set(), ("link", 0, 1)
+    moved, also, soon, due, long, LINK = {}, {}, {}, {}, set(), ("link", 0, 1)
 
     def regs(views):
         return [r for x in views for r in x[1]]
@@ -152,7 +166,7 @@ def rank_program(g, core, T, topo):
         touched, before = {}, []
         for j, (q, f, reads, writes, t, lat) in enumerate(calls):
             dep = set()
-            for rs, w in ((reads, False), (writes, True)):
+            for rs, w in ((reads, False), (writes + also.get(j, []), True)):
                 for (k, lo, hi) in rs:
                     dep |= {i for (l2, h2, w2, i) in touched.get(k, []) if (l2 < hi and lo < h2 and (w or w2)) or (k in BANKS and q == "t" == calls[i][0])}
             before.append(dep)
@@ -167,7 +181,7 @@ def rank_program(g, core, T, topo):
         def gap(i, j, early=0):
             if LINK in calls[i][3] and LINK in calls[j][3]:
                 return COST["link"] * (calls[i][3][0][0] == "land")
-            if ("turn", 0, 1) in calls[i][3] and ("turn", 0, 1) in calls[j][3]:
+            if any((k, 0, 1) in calls[i][3] and (k, 0, 1) in calls[j][3] for k in ("turn", "fold")):
                 return 0.0
             return 0.0 if calls[i][0] == calls[j][0] == "t" else calls[i][5] + moved.get(i, 0.0) + early * soon.get(i, 0.0)
         banks = [{k for (k, lo, hi) in c[2] + c[3] if k in BANKS} for c in calls]
@@ -243,12 +257,14 @@ def rank_program(g, core, T, topo):
     def mm(out, lhs, rhs, start, stop):
         op("t", lambda: g.tensor.matmul(out[0], lhs[0], rhs[0], start, stop), [out], [lhs, rhs])
 
+    def run(mms):
+        def f():
+            for (out, lhs, rhs, start, stop) in mms:
+                now("t", lambda: g.tensor.matmul(out[0], lhs[0], rhs[0], start, stop), [out], [lhs, rhs])
+        calls.append(("t", f, regs([x for m in mms for x in m[1:3]]), regs([m[0] for m in mms]), sum(COST["mm"] * max(64, m[0][2]) for m in mms), COST["wait"]))
+
     def back(out, z, src, a, b):
-        def run():
-            for i in range(16):
-                lhs, rhs = V2(z, 15 - i, 143 - i), V2(src, a + i, b, 16)
-                now("t", lambda: g.tensor.matmul(out[0], lhs[0], rhs[0], i == 0, i == 15), [out], [lhs, rhs])
-        calls.append(("t", run, V2(z)[1] + V2(src, a, b)[1], out[1], 16 * COST["mm"] * max(64, out[2]), COST["wait"]))
+        run([(out, V2(z, 15 - i, 143 - i), V2(src, a + i, b, 16), i == 0, i == 15) for i in range(16)])
 
     def aff(out, a, pat, cmp, base, cm):
         op("g", lambda: g.affine_select(out[0], a[0], pat, cmp, 0.0, base, cm), [out], [a])
@@ -268,8 +284,9 @@ def rank_program(g, core, T, topo):
     def dma(q, out, a, after=()):
         size = max(out[2] * (4 if out[1] and wide(out) else 2), a[2] * (4 if a[1] and wide(a) else 2))
         moved[len(calls)] = COST["byte"] * size
+        also[len(calls)] = list(after)
         soon[len(calls)] = SOON.get(out[1][0][0], 0.0) if out[1] else 0.0
-        calls.append((q, lambda: dma_now(q, out, a, list(after)), a[1] + list(after), out[1], COST["dma"], COST["load"]))
+        calls.append((q, lambda: dma_now(q, out, a, list(after)), list(a[1]), list(out[1]), COST["dma"], COST["load"]))
 
     def hbm(ap):
         return (ap, [], 0)
@@ -300,7 +317,7 @@ def rank_program(g, core, T, topo):
         a, b = topo.chip(T.cores[0]), topo.chip(T.cores[d])
         return 2 if topo.mates(a, b) else 1 if topo.same_plane(a, b) else 0
 
-    DIST = sorted(range(1, N), key=hops)
+    DIST = sorted(range(1, N), key=lambda d: (hops(d), (d // 4 + hops(d) + 1) % 2))
     DIST.insert(S0, 0)
     owner = [me ^ d for d in DIST]
     asker = owner
@@ -326,6 +343,7 @@ def rank_program(g, core, T, topo):
     dma("y", V2("thrI"), hbm(T.thr[:]), V2("sdI")[1])
     dma("y", V2("aliI"), hbm(T.ali[:]), V2("sdI")[1])
     dma("y", V2("seenS"), hbm(T.seen[:]), V2("rkI")[1])
+    dma("y", V2("vecS", 0, 1024), hbm(T.vec[:, 0:1024]), V2("seenS")[1])
 
     fill(V2("oneb"), 1.0)
     fill(V2("rst"), 1.0)
@@ -342,7 +360,8 @@ def rank_program(g, core, T, topo):
     iota(V2("iotaC"), [[1597, 4], [7985, 4], [0, 16]], 1597 + 2048, 0, True)
     aff(V2("Id"), V2("oneb", 0, 128), [[-1, 128]], A.is_equal, 0, 1)
     aff(V2("Tri"), V2("BD"), [[1, 128]], A.is_gt, 0, -1)
-    iota(V2("W1"), [[128, 16], [0, 128]], 0, 0, True)
+    for z in range(3):
+        iota(V2("Vwin", 512 * z, 512 * z + 512), [[0, 512]], 0, 0, True)
     fill(V2("rst", 0, 512, 64), 0.0)
     fill(V2("Zs"), 0.0)
     ts(V2("pm"), V2("pI"), 15, None, A.bitwise_and)
@@ -382,23 +401,27 @@ def rank_program(g, core, T, topo):
         tt(V2("Zk"), V2("w12"), V2("Bq"), A.add)
         cp(V2("I1"), V2("Id"))
         op("s", lambda: g.scalar.activation(T.dH[:, 0:7], T.dB[:, 0:7], F.Copy, scale=0.5, accum_out=T.dH[:, 7:8]), [V2("dH")], [V2("dB")])
+        dg = [V2("W1", 1024 + 128 * w, 1152 + 128 * w) for w in range(8)]
         for w in range(8):
-            act(V2("Dg", 128 * w, 128 * w + 128), IdM, scale=V2("dH", w, w + 1))
-        mm(own, V2("Dg", 896, 1024), V2("oneb", 0, 64), True, False)
+            act(dg[w], IdM, scale=V2("dH", w, w + 1))
+        mm(own, dg[7], V2("oneb", 0, 64), True, False)
+        fill(V2("W1", 960, 1024), 0.0)
         for w in range(8):
-            ts(V2("stp", 128 * w, 128 * w + 64), V2("Zk"), V2("tA", w, w + 1), V2("dA", w, w + 1), A.is_ge, A.mult)
-            mm(own, IdM, V2("stp", 128 * w, 128 * w + 64), False, w == 7)
+            ts(V2("W1", 128 * w, 128 * w + 64), V2("Zk"), V2("tA", w, w + 1), V2("dA", w, w + 1), A.is_ge, A.mult)
+            mm(own, IdM, V2("W1", 128 * w, 128 * w + 64), False, w == 7)
             if w < 7:
-                act(V2("stp", 128 * w + 64, 128 * w + 128), V2("Zk"), F.Sign, bias=0.5 - 4096.0 * (w + 1))
-                mm(own, V2("Dg", 128 * w, 128 * w + 128), V2("stp", 128 * w + 64, 128 * w + 128), False, False)
+                act(V2("W1", 128 * w + 64, 128 * w + 128), V2("Zk"), F.Sign, bias=0.5 - 4096.0 * (w + 1))
+                mm(own, dg[w], V2("W1", 128 * w + 64, 128 * w + 128), False, False)
         for s in range(N):
             ts(V2("b2", 64 * s, 64 * s + 64), own, float(owner[s]), None, A.is_equal)
-        scan(V2("Pc"), V2("rst"), V2("b2"), A.mult, A.add)
+        for a in range(0, 512, SC):
+            scan(V2("Pc", a, a + SC), V2("rst", a, a + SC), V2("b2", a, a + SC), A.mult, A.add)
         act(V2("ownb"), own)
         mm(V2("b4", 24, 32), IdM, V2("s256"), True, False)
         mm(V2("b4", 24, 32), V2("Tri"), cnt, False, True)
         mm(V2("b1", 256, 264), V2("Tri"), cnt, True, True)
-        tt(V2("Dc"), V2("Pc"), V2("b2"), A.mult)
+        for a in range(0, 512, SC):
+            tt(V2("Dc", a, a + SC), V2("Pc", a, a + SC), V2("b2", a, a + SC), A.mult)
         for s in range(N):
             mm(f2, IdM, V2("Dc", 64 * s, 64 * s + 64), s == 0, False)
         for s in range(N):
@@ -441,63 +464,100 @@ def rank_program(g, core, T, topo):
                 dma("y", row("VxS", v), V2("hv", 64 * v, 64 * v + 64), [("VxS", 0, 1024)])
 
     def scatter():
-        iota(V2("jc"), [[16, LC], [0, 3], [1, 16]], 0, 0, True, [V3("rnS", 0, N, 0, 1)])
+        send([(s, owner[s], V3("rnS", s, s + 1, 0, 2), T.rn[:, s, :]) for s in FAR], "rn")
+        calls[-1][3].append(("turn", 0, 1))
+        iota(V2("jc"), [[16, LC], [0, 3], [1, 16]], 0, 0, True)
+        calls[-1][3].append(("turn", 0, 1))
         iota(V2("p4"), [[1, 128]], 0, 0, True)
         aff(V2("Za"), V2("Zs"), [[-16, 9], [0, 16]], A.is_ge, 0, 1)
+        calls[-1][3].append(("turn", 0, 1))
         aff(V2("Zt"), V2("Za"), [[16, 9], [0, 16]], A.is_ge, 2, -1)
         aff(V2("Zs"), V2("Za"), [[16, 9], [0, 16]], A.is_ge, 15, -1)
         fill(E("sI", 0, N, 0, 1), 0)
         aff(V2("Zi"), V2("Zs"), [[-16, 9], [0, 16]], A.is_ge, -3, 1)
         aff(V2("Zi"), V2("Zi"), [[16, 9], [0, 16]], A.is_ge, 4, -1)
-        send([(s, owner[s], (T.rnS[:, s, :], V3("rnS", s, s + 1, 0, 2)[1] + V2("hv")[1], 2), T.rn[:, s, :]) for s in FAR], "rn")
-        for z in range(3):
-            act(V2("Vwin", 512 * z, 512 * z + 512), V2("rst"), scale=0.0)
-            calls[-1][2].extend(V2("hb")[1])
+        dma("y", V2("vecS", 1024, 2048), (T.vec[:, 1024:2048], rows("VxS")[1], 0))
         cp(IX(V2("Vwin"), V2("F2u")), rows("VxS"))
         for v in range(4):
-            dma("y", V2("fv", 96 * v, 96 * v + 96), (T.Vwin[v:128:16, :], V2("Vwin")[1], 96))
+            dma(FQ[v % 2], V2("fv", 96 * v, 96 * v + 96), (T.Vwin[v:128:16, :], V2("Vwin")[1], 96))
+            calls[-1][3].append(("fold", 0, 1))
 
     def lists():
         for i in range(4):
             ts(V2("b6", 96 * i, 96 * i + 96), V2("fv", 96 * i, 96 * i + 96), 1.5 * 2 ** 35, 1.5 * 2 ** 35, A.add, A.subtract)
         for i in range(4):
-            le, msg = ((T[nm][:, :, 3 - i:48:4], [(nm, 48 * s + 3 - i, 48 * s + 4 - i) for s in range(N)], N * LC) for nm in ("le", "msg"))
+            x = slice(0, LC) if i == 3 else slice(LC + 2 - i, 48, 3)
+            le, msg = ((T[nm][:, :, x], [(nm, 48 * s + x.start, 48 * s + x.start + 1) for s in range(N)], N * LC) for nm in ("le", "msg"))
             y, r = V2("fv", 96 * i, 96 * i + 96), V2("b6", 96 * i, 96 * i + 96)
             tt(le, y, r, A.subtract)
             calls[-1][2].extend(V2("b6", 96 * LT, 96 * LT + 96)[1])
             act(msg, y, F.Identity, bias=2048.0)
+            calls[-1][2].extend(V2("seenD", 0, MS)[1])
         act(V3("rq", S0, S0 + 1, 0, 48), V3("msg", S0, S0 + 1, 0, 48))
         for m, k in SENDS:
             send([(s, owner[s], V3("le" if m == "rl" else "msg", s, s + 1, 0, 48), T.rl[:, 48 * s:48 * s + 48] if m == "rl" else T.rq[:, s, :]) for s in GRP[k]], m)
             calls[-1][3].append(("turn", 0, 1))
-        dma("y", V2("vecS"), hbm(T.vec[:]), LAND["rl"](0)[1])
 
-    def piece(j):
-        dma("y", row("W1", j), V2("p%d" % j), [("W1", 0, 2048)])
+    def table():
+        for j in (3, 4, 0, 1, 2):
+            dma("y", row("W1", j), V2("p%d" % j), V2("W1")[1])
+            calls[-1][3].extend([("fold", 0, 1)] * (j < 3))
 
     def pieces():
-        piece(4)
+        ts(V2("c0", 2, 3), V2("pm"), 128.0, None, A.mult)
+        act(V2("p3"), V2("oneb", 0, 128), scale=V2("c0", 2, 3))
         t0, t1, t2 = (V2(PB, 128 * z, 128 * z + 128) for z in (1, 2, 3))
         ts(t0, V2("thrI"), 4096.0, None, A.mult)
         tt(t1, V2("aliI"), t0, A.add)
-        act(V2("p0"), t1)
+        cp(V2("p0"), t1)
+        calls[-1][2].extend(V2("Vwin")[1])
         tt(t2, t1, V2("p0"), A.subtract)
-        act(V2("p1"), t2)
+        cp(V2("p1"), t2)
         tt(V2("p2"), t2, V2("p1"), A.subtract)
-        for j in range(3):
-            piece(j)
     tab = rows("W1")
 
-    def masks():
-        act(V2("Md"), V2("BD"), scale=-1.0)
-        aff(V2("Md"), V2("Md"), [[1, 128]], A.is_equal, -1, -1)
+    def tables():
+        def M(k):
+            return V2("Md", 128 * k, 128 * k + 128)
+        act(M(0), V2("BD"), scale=-1.0)
+        aff(M(0), M(0), [[1, 128]], A.is_equal, -1, -1)
+        op("g", lambda: g.affine_select(M(0)[0], M(0)[0], [[-1, 128]], A.not_equal, 1.0, 0, 1), [M(0)], [M(0)])
+        for k, a, c in ((1, M(0), 16.0), (2, M(0), 1.0 / 16), (3, IdM, -16.0)):
+            act(M(k), a, scale=c)
+            due[len(calls) - 1] = 26.0
+        ts(V2("c0", 1, 2), V2("pmF"), 0.0, -17.0 * 192, A.is_equal, A.mult)
+        for z in range(2):
+            dma("y", V2("aliJ", 64 * z, 64 * z + 64), hbm(T.ali[:, 1024 * z:1024 * z + 1024]), V2("rkI")[1])
+        cp(V2("aliU"), V2("aliJ"))
+        for o in range(0, 2048, HW):
+            if o < HV:
+                ts(V2("hS", o, o + HW), V2("seenS", o, o + HW), 3072 - 7.5, None, A.add)
+            else:
+                act(V2("hS", o, o + HW), V2("seenS", o, o + HW), F.Identity, bias=3072 - 7.5)
+                calls[-1][2].extend(V2("hb")[1])
         for z in range(4):
-            mm(V2(TB[z % 2]), IdM, V2("seenS", 512 * z, 512 * z + 512), True, False)
-            calls[-1][2].extend(V2("fh")[1])
-            mm(V2(TB[z % 2]), V2("Md"), V2("seenS", 512 * z, 512 * z + 512), False, True)
-            act(V2("seenD", 512 * z, 512 * z + 512), V2(TB[z % 2]))
+            act(V2("sA", 512 * z, 512 * z + 512), IX(V2("seenS"), V2("aliU", 32 * z, 32 * z + 32)))
+            calls[-1][2].extend(V3("rnS", 0, N, 0, 1)[1] if z >= RZ else V2("hb")[1])
+            act(V2("hA", 512 * z, 512 * z + 512), V2("sA", 512 * z, 512 * z + 512), F.Identity, bias=3072 - 7.5)
+        for n, (h, k, nm, ka, na) in enumerate(((1, 2, "hS", 0, "hA"), (0, 0, "seenS", 1, "sA"))):
+            for z in range(4):
+                bank, o = HB[4 * n + z], 1024 * (z // 2)
+                mm(V2(bank), M(k), V2(nm, 512 * z, 512 * z + 512), True, False)
+                calls[-1][2].extend(V2("fh")[1])
+                run([(V2(bank, 64 * p, 64 * p + 64), M(ka), V2(na, o + 8 * (z % 2) + p, o + 1024, 16), False, h == 1 and p == 7) for p in range(8)])
+                if not h:
+                    mm(V2(bank), M(3), V2("seenD", 2048 + 512 * z, 2560 + 512 * z), False, True)
+                o = V2("seenD", 2048 * h + 512 * z, 2048 * h + 512 * z + 512)
+                if 4 * n + z in EV:
+                    cp(o, V2(bank))
+                    calls[-1][2].extend(V2("Vwin")[1])
+                else:
+                    act(o, V2(bank), F.Identity, bias=V2("c0", 1, 2) if h else 0.0)
+                due[len(calls) - 1] = DUT[n] - 0.1 * z
+
+    def masks():
         for s in range(N):
-            ts(V2("mk", 576 * s, 576 * s + 576), V2("jc"), V3("rnS" if s == S0 else "rn", s, s + 1, 0, 1), float(2 ** (20 - asker[s])), A.is_ge, A.mult)
+            ts(V2("mk", 576 * s, 576 * s + 576), V2("jc"), V3("rnS" if s == S0 else "rn", s, s + 1, 0, 1), float(2 ** (16 - asker[s] % 4)), A.is_ge, A.mult)
             calls[-1][2].extend(V2("Vwin")[1] if s in MK else V3("le", 0, N, 0, 48)[1])
 
     def ylist():
@@ -508,45 +568,53 @@ def rank_program(g, core, T, topo):
     def look(c):
         a, b = CH[c]
         for s in range(a, b):
-            for f, u, v in ((cp, 0, GV.get(s, 0)), (act, GV.get(s, 0), 48)):
+            for f, u, v in [(cp, u, min(u + GW, GV[s])) for u in range(0, GV.get(s, 0), GW)] + [(act, GV.get(s, 0), 48)]:
                 if u < v:
                     lst = (T.le[:, s, u:v], V3("le", s, s + 1, 0, 48)[1], v - u) if s == S0 else V2("rl", 48 * s + u, 48 * s + v)
                     f(V2("GT", 768 * s + 16 * u, 768 * s + 16 * v), IX(tab, lst))
 
     def arrive(c):
         a, b = CH[c]
-        back(V2(TB[c % 3], 0, 48 * (b - a)), "Zt", "GT", 768 * a, 768 * b)
+        back(V2(TB[c], 0, 48 * (b - a)), "Zt", "GT", 768 * a, 768 * b)
 
     def filt(c):
         a, b = CH[c]
-        tt(V3("mn", a, b, 0, 48), V3("rq", a, b, 0, 48), V2(TB[c % 3], 0, 48 * (b - a)), A.min)
-        ts(E("cI", a, b, 0, 4), V3("mn", a, b, 0, 48), 2047, None, A.bitwise_and)
-        cp(V2("ls", 36 * a, 36 * b), E("cI", a, b, 1, 4))
+        tt(V3("mn", a, b, 0, 48), V3("rq", a, b, 0, 48), V2(TB[c], 0, 48 * (b - a)), A.min)
+        tt(V3("fl", a, b, 0, 48), V3("rq", a, b, 0, 48), V2(TB[c], 0, 48 * (b - a)), A.is_lt)
+        ts(E("cI", a, b, 0, 1), V3("mn", a, b, 0, LC), 2047, None, A.bitwise_and)
+        ts(E("cI", a, b, 1, 4), V3("mn", a, b, LC, 48), 2047, None, A.bitwise_and)
+        ts(V2("fac", 36 * a, 36 * b), V3("fl", a, b, LC, 48), 15.0, 1.0, A.mult, A.add)
         w = MGW[c]
-        for o in range(36 * a, 36 * b, w):
-            tt(V2("MG", 16 * o, 16 * (o + w)), IX(V2("seenD"), V2("ls", o, o + w)), V2("mk", 16 * o, 16 * (o + w)), A.mult)
-            due[len(calls) - 1] = DUE[c][0]
-            long.add(len(calls) - 1)
-        back(V2("b%d" % (2 + c % 2), 0, 36 * (b - a)), "Zs", "MG", 576 * a, 576 * b)
+        for s in range(a, b):
+            for u in range(0, 36, w):
+                o, h = 36 * s + u, 2048 * (asker[s] // 4)
+                lst = (T.le[:, s, LC + u:LC + u + w], V3("le", s, s + 1, 0, 48)[1], w) if s == S0 else V2("rl", 48 * s + LC + u, 48 * s + LC + u + w)
+                tt(V2("MG", 16 * o, 16 * (o + w)), IX(V2("seenD", h, h + 2048), lst), V2("mk", 16 * o, 16 * (o + w)), A.mult)
+                due[len(calls) - 1] = DUE[c]
+                long.add(len(calls) - 1)
 
     def pick(c):
-        a, b = CH[c]
+        a, b = PG[c]
         w, x = (48 * a, 48 * b), (LC * a, LC * b)
-        cp(E("sI", a, b, 1, 4), V2("b%d" % (2 + c % 2), 0, 36 * (b - a)))
+        back(V2(FB[c], 0, 36 * (b - a)), "Zs", "MG", 576 * a, 576 * b)
+        tt(E("sI", a, b, 1, 4), V2("fac", 36 * a, 36 * b), V2(FB[c], 0, 36 * (b - a)), A.mult)
         ts(V2("sb", *w), E("sI", a, b, 0, 4), 2 ** 20, None, A.bitwise_and)
         tt(V2("kb", *w), E("cI", a, b, 0, 4), V2("sb", *w), A.subtract)
         scan(V2("kc", *w), V2("sb", *w), V2("kb", *w), A.min, A.max)
         cp(V2("lx", *x), V2("kc", 48 * a + 3, 48 * b, 4))
-        due[len(calls) - 1] = DUE[c][1]
+        due[len(calls) - 1] = DUP[c]
         far = [s for s in range(a, b) if s != S0]
         if far:
             act(V2("rs", CAPQ * far[0], CAPQ * far[-1] + CAPQ), IX(V2("vecS"), V2("lx", LC * far[0], LC * far[-1] + LC)))
         if a <= S0 < b:
             act(V2("land", SW * S0, SW * S0 + CAPQ), IX(V2("vecS"), V2("lx", LC * S0, LC * S0 + LC)))
-        for gr in GRP:
-            if a <= gr[0] < b:
-                send([(s, asker[s], V2("lx", LC * s, LC * s + LC), T.lr[:, LC * s:LC * s + LC]) for s in gr], "lr")
-                send([(s, asker[s], V2("rs", CAPQ * s, CAPQ * s + CAPQ), T.land[:, SW * s:SW * s + CAPQ]) for s in gr], "la")
+
+    def answers():
+        for m, k in BACK:
+            if m == "lr":
+                send([(s, asker[s], V2("lx", LC * s, LC * s + LC), T.lr[:, LC * s:LC * s + LC]) for s in GRP[k]], m)
+            else:
+                send([(s, asker[s], V2("rs", CAPQ * s, CAPQ * s + CAPQ), T.land[:, SW * s:SW * s + CAPQ]) for s in GRP[k]], m)
 
     def items(c):
         for s in range(*CH[c]):
@@ -554,14 +622,17 @@ def rank_program(g, core, T, topo):
             if s in IL:
                 held.append(calls[-1])
 
-    for f in (owners, cands, scatter, pieces, ylist, lists):
+    for f in (owners, cands, scatter, pieces, ylist, tables, lists, masks):
         f()
-    masks()
-    for c in ORDER:
-        for f in (look, arrive, filt, pick):
+    table()
+    for c in range(len(CH)):
+        for f in (look, arrive, filt):
             f(c)
+    for c in range(len(PG)):
+        pick(c)
+    answers()
     held = []
-    for c in ORDER:
+    for c in range(len(CH)):
         items(c)
     for x in held:
         x[2].extend(V2("rs" if x[0] == "s" else "lx")[1])

from concourse.bass import DstId, RemoteDMATransfer
from concourse.mybir import AluOpType, ActivationFunctionType

A = AluOpType
F = ActivationFunctionType
N = 8
CAPQ, LC, SW = 192, 12, 192
S0 = 7
CH = [(0, 2), (2, 4), (4, 6), (6, 7), (7, 8)]
PG = [(0, 2), (2, 4), (4, 6), (6, 8)]
GRP = [(0, 1), (2, 3), (4, 5), (6,)]
DUE = [16.2, 14.1, 11.8, 8.7, 11.0]
DUP = [14.2, 11.5, 8.4, 8.5]
DUT = [21.0, 17.0]
EV = ()
HW = 256
RZ = 1
MS = 1536
HV = 2048
HB = ["b0", "b1", "b2", "b3", "b7", "b4", "b0", "b1"]
HO = [0, 1, 4, 5, 2, 3, 6, 7]
COST = {"cycle": 0.00085, "gather": 0.0013, "scatter": 0.0031, "mm": 0.00059, "wait": 0.207, "dma": 0.08, "load": 0.98, "byte": 0.0004, "call": 0.35, "far": 1.43, "first": 1.8, "link": 1.0}
AHEAD, TURNS = 0.2, 1
SOON = {"rn": 4.5, "W1": 1.0, "VxS": 0.0}
MGW = [36, 36, 18, 12, 12]
PARTS = 4
ROW = 1 << 16
GV = {7: 24}
IV = (2, 4, 6)
IL = (2, 3, 4, 5, 6)
SENDS = [("rl", 0), ("rl", 1), ("rq", 0), ("rl", 2), ("rq", 1), ("rl", 3), ("rq", 2), ("rq", 3)]
BACK = [("lr", 0), ("la", 0), ("lr", 1), ("la", 1), ("lr", 2), ("lr", 3), ("la", 2), ("la", 3)]
YP = 4
LT = 2
SC = 128
GW = 24
FQ = "yy"
SHORT = 1.0
MK = (0, 1, 2, 3)
PB = "b5"
TB = ["b7", "b4", "b0", "b1", "b5"]
FB = ["b2", "b3", "b2", "b3", "b6"]
f32, b16, i32, u16, f16 = "float32", "bfloat16", "int32", "uint16", "float16"
SHAPES = {
    i32: {"sdI": 1, "rkI": 16, "thrI": 128, "aliI": 128, "aliJ": 128, "iotaK": 64, "pI": 1, "pm": 1, "pg": 1,
          "loI": 1, "hiI": 1, "Lr": 64, "Lq": 64, "t1": 64, "Bq": 64, "Lp": 64, "t2": 64, "w12": 64, "fh": 64,
          "hx": 256, "hL": 256, "ht": 256, "hB": 256, "hu": 256, "he": 256,
          "mn": (8, 48), "cI": (96, 4), "sI": (96, 4), "sb": 384},
    f32: {"rkF": 16, "BDf": 128, "w1c": 8, "w4c": 8, "sdF": 1, "pgF": 1, "iotaC": 256, "hpF": 1, "Zk": 64, "tA": 8, "dA": 8, "dB": 8, "dH": 8,
          "pmF": 1, "cxF": 1, "nC": 256, "loC": 1, "hiC": 1, "hv": 256, "fa": 64, "Lf": 256, "Bf": 256, "hq": 256, "hb": 256,
          "VxS": 1024, "Vwin": 1536, "fv": 384, "own2k": 64, "c0": 3, "fl": (8, 48), "fac": 288,
          "msg": (8, 48), "rq": (8, 48), "chS": 64, "kb": 384, "kc": 384},
    b16: {"seenS": 2048, "vecS": 2048, "W1": 2048, "oneb": 256, "gC": 128, "Gc": 128, "Id": 128, "Tri": 128, "BD": 128, "rst": 512, "uC": 256, "s256": 8,
          "Zs": 144, "Za": 144, "Zt": 144, "Zi": 144, "jc": 576, "p3": 128, "Pc": 512, "Dc": 512, "ownb": 64,
          "p0": 128, "p1": 128, "p2": 128, "p4": 128, "rs": 1536, "land": 1536, "seenD": 4096, "Md": 640, "hS": 2048, "sA": 2048, "hA": 2048, "rnS": (8, 2), "rn": (8, 2), "mk": 4608, "GT": 6144, "MG": 4608,
          "IDx": 1536, "IDg": 1024, "yS": 1024},
    u16: {"F2u": 64, "yo": 64, "le": (8, 48), "rl": 384, "lx": 96, "lr": 96, "aliU": 128},
    f16: {"I1": 128, "G1": 128, "G64": 128, "Rlo": 256, "Rhi": 256, "Of": 512},
}
SCRATCH = {}
for _dt, _d in SHAPES.items():
    for _k, _n in _d.items():
        SCRATCH[_k] = ("sbuf", [128] + (list(_n) if isinstance(_n, tuple) else [_n]), _dt)
for _b in range(8):
    SCRATCH["b%d" % _b] = ("psum", [128, 512], f32)
SEMAPHORES = ["sv", "ss", "st", "sg", "lsem"] + ["d%d" % _k for _k in range(40)] + ["%s%d" % (_m, _k) for _m in ("rn", "rl", "rq", "lr", "la") for _k in range(N)]


def rank_program(g, core, T, topo):
    me = T.rank_of(core)
    if me is None:
        return
    queue = {"v": g.vector, "s": g.scalar, "t": g.tensor, "g": g, "y": g.sync}
    count = {}
    clock = {q: {} for q in queue}
    seen_by = {}
    log = {}
    ndma = [0]

    def V2(name, a=0, b=None, step=1, p=None):
        b = SCRATCH[name][1][1] if b is None else b
        ap = T[name][:, a:b:step] if p is None else T[name][p, a:b:step]
        return (ap, [(name, a, b)], len(range(a, b, step)))

    def V3(name, s0, s1, a, b):
        w = SCRATCH[name][1][2]
        ap = T[name][:, s0, a:b] if s1 == s0 + 1 else T[name][:, s0:s1, a:b]
        return (ap, [(name, s * w + a, s * w + b) for s in range(s0, s1)], (s1 - s0) * (b - a))

    def E(name, s0, s1, a, b):
        w = SCRATCH[name][1][2]
        ap = T[name][:, LC * s0:LC * s1, a] if b == a + 1 else T[name][:, LC * s0:LC * s1, a:b]
        return (ap, [(name, s * w + a, s * w + b) for s in range(s0, s1)], (s1 - s0) * LC * (b - a))

    def IX(win, off):
        return (win[0].indirect(off[0]), win[1] + off[1], 16 * off[2], True)

    def row(nm, v):
        return (T[nm][v:128:16, :], [(nm, ROW + v, ROW + v + 1)], SCRATCH[nm][1][1] // 16)

    def rows(nm):
        return (T[nm][:], [(nm, 0, ROW + 16)], SCRATCH[nm][1][1])

    BANKS = ["b%d" % k for k in range(8)]

    def need(q, reads, writes):
        toks = []
        for rs, w in ((reads, False), (writes, True)):
            for (k, lo, hi) in rs:
                for (l2, h2, w2, tok, e2) in log.get(k, []):
                    if k in BANKS and e2 != q:
                        toks.append(tok)
                    elif l2 < hi and lo < h2 and (w or w2) and not (q == "t" and e2 == "t"):
                        toks.append(tok)
        best = {}
        for (s, n) in toks:
            if clock[q].get(s, 0) < n:
                best[s] = max(best.get(s, 0), n)
        for s in sorted(best, key=lambda s: (s[0] != "d", s)):
            n = best[s]
            if clock[q].get(s, 0) < n:
                queue[q].wait_ge(T.sem[s], n)
                clock[q][s] = n
                for s2, n2 in seen_by.get((s, n), {}).items():
                    clock[q][s2] = max(clock[q].get(s2, 0), n2)

    def done(q, inst, reads, writes, sem, inc):
        inst.then_inc(T.sem[sem], inc)
        count[sem] = count.get(sem, 0) + inc
        tok = (sem, count[sem])
        c = dict(clock[q])
        c[sem] = count[sem]
        seen_by[tok] = c
        for rs, w in ((reads, False), (writes, True)):
            for (k, lo, hi) in rs:
                log.setdefault(k, []).append((lo, hi, w, tok, q))

    calls = []
    moved, also, soon, due, long, LINK = {}, {}, {}, {}, set(), ("link", 0, 1)

    def regs(views):
        return [r for x in views for r in x[1]]

    def now(q, f, outs, ins):
        need(q, regs(ins), regs(outs))
        done(q, f(), regs(ins), regs(outs), "s" + q, 1)

    def wide(x):
        return SCRATCH[x[1][0][0]][2] in (f32, i32)

    def op(q, f, outs, ins, cyc=1.0):
        n = outs[0][2]
        if len(outs[0]) > 3:
            t = 0.05 + COST["scatter"] * ins[0][2]
        elif ins and len(ins[0]) > 3:
            t = 0.06 + COST["gather"] * n
        elif q == "t":
            t = COST["mm"] * max(64, n) * (4 if wide(ins[0]) else 1)
        elif q == "g":
            t = 0.15 + 2 * COST["cycle"] * n
        else:
            t = COST["cycle"] * max(64, n * cyc * (0.5 if q == "v" and not any(wide(x) for x in outs + ins) else 1))
        calls.append((q, lambda: now(q, f, outs, ins), regs(ins), regs(outs), t, COST["wait"]))

    def issue():
        touched, before = {}, []
        for j, (q, f, reads, writes, t, lat) in enumerate(calls):
            dep = set()
            for rs, w in ((reads, False), (writes + also.get(j, []), True)):
                for (k, lo, hi) in rs:
                    dep |= {i for (l2, h2, w2, i) in touched.get(k, []) if (l2 < hi and lo < h2 and (w or w2)) or (k in BANKS and q == "t" == calls[i][0])}
            before.append(dep)
            for rs, w in ((reads, False), (writes, True)):
                for (k, lo, hi) in rs:
                    touched.setdefault(k, []).append((lo, hi, w, j))
        after = [[] for c in calls]
        for j, dep in enumerate(before):
            for i in dep:
                after[i].append(j)

        def gap(i, j, early=0):
            if LINK in calls[i][3] and LINK in calls[j][3]:
                return COST["link"] * (calls[i][3][0][0] == "land")
            if any((k, 0, 1) in calls[i][3] and (k, 0, 1) in calls[j][3] for k in ("turn", "fold")):
                return 0.0
            return 0.0 if calls[i][0] == calls[j][0] == "t" else calls[i][5] + moved.get(i, 0.0) + early * soon.get(i, 0.0)
        banks = [{k for (k, lo, hi) in c[2] + c[3] if k in BANKS} for c in calls]

        def deal(way, before, after, back):
            left = [len(d) for d in before]
            ready = {j: gap(j, j) if back else 0.0 for j in range(len(calls)) if not left[j]}
            free = {q: 0.0 for q in list(queue) + ["dma"]}
            bank, late, order, end = {}, {}, [], [0.0] * len(calls)
            while ready:
                st = {j: max([ready[j], free[calls[j][0]]] + [bank[k][1] for k in banks[j] if k in bank and bank[k][0] != calls[j][0]]) for j in ready}
                first = min(ready, key=lambda j: (st[j], -way[j], j))
                j = min((i for i in ready if calls[i][0] == calls[first][0] and st[i] <= st[first] + min(AHEAD * calls[first][4], 0.5)), key=lambda i: (SHORT * (i in long) - way[i], i))
                q = calls[j][0]
                order.append(j)
                free[q] = end[j] = st[j] + calls[j][4]
                held = 0.0
                if j in moved and not back:
                    held = max(0.0, free["dma"] - free[q])
                    free["dma"] = free[q] + held + moved[j]
                for k in banks[j]:
                    bank[k] = (q, free[q] + COST["wait"])
                del ready[j]
                for k in after[j]:
                    left[k] -= 1
                    late[k] = max(late.get(k, 0.0), free[q] + held + (gap(k, j, 1) if back else gap(j, k)))
                    if not left[k]:
                        ready[k] = late[k]
            return order, end
        way = [0.0] * len(calls)
        for j in reversed(range(len(calls))):
            way[j] = calls[j][4] + max([gap(j, k, 1) + way[k] for k in after[j]] + [calls[j][5], due.get(j, 0.0)])
        best = None
        for turn in range(TURNS):
            order, end = deal(way, before, after, False)
            if best is None or max(end) < best[0]:
                best = (max(end), order)
            way = deal(end, after, before, True)[1]
        for j in best[1]:
            calls[j][1]()

    def isv(x):
        return isinstance(x, tuple)

    def raw(x):
        return x[0] if isv(x) else x

    def ts(out, in0, s1, s2, o0, o1=None):
        ins = [x for x in (in0, s1, s2) if isv(x)]
        if o1 is None:
            op("v", lambda: g.vector.tensor_scalar(out[0], in0[0], raw(s1), None, o0), [out], ins)
        else:
            op("v", lambda: g.vector.tensor_scalar(out[0], in0[0], raw(s1), raw(s2), o0, o1), [out], ins)

    def tt(out, a, b, o):
        cyc = 1 if a[1][0][0] in BANKS or b[1][0][0] in BANKS else 2 if wide(out) or wide(a) or wide(b) else 4
        op("v", lambda: g.vector.tensor_tensor(out[0], a[0], b[0], o), [out], [a, b], cyc)

    def scan(out, a, b, o0, o1):
        op("v", lambda: g.vector.tensor_tensor_scan(out[0], a[0], b[0], 0.0, o0, o1), [out], [a, b])

    def cp(out, a):
        op("v", lambda: g.vector.tensor_copy(out[0], a[0]), [out], [a])

    def fill(out, c):
        op("v", lambda: g.vector.memset(out[0], c), [out], [])

    def act(out, a, func=F.Copy, **kw):
        ins = [a] + [x for x in kw.values() if isv(x)]
        k2 = {k: raw(x) for k, x in kw.items()}
        op("s", lambda: g.scalar.activation(out[0], a[0], func, **k2), [out], ins)

    def mm(out, lhs, rhs, start, stop):
        op("t", lambda: g.tensor.matmul(out[0], lhs[0], rhs[0], start, stop), [out], [lhs, rhs])

    def run(mms):
        def f():
            for (out, lhs, rhs, start, stop) in mms:
                now("t", lambda: g.tensor.matmul(out[0], lhs[0], rhs[0], start, stop), [out], [lhs, rhs])
        calls.append(("t", f, regs([x for m in mms for x in m[1:3]]), regs([m[0] for m in mms]), sum(COST["mm"] * max(64, m[0][2]) for m in mms), COST["wait"]))

    def back(out, z, src, a, b):
        run([(out, V2(z, 15 - i, 143 - i), V2(src, a + i, b, 16), i == 0, i == 15) for i in range(16)])

    def aff(out, a, pat, cmp, base, cm):
        op("g", lambda: g.affine_select(out[0], a[0], pat, cmp, 0.0, base, cm), [out], [a])

    def iota(out, pat, base, cm, small=False, after=()):
        if small:
            op("g", lambda: g.iota(out[0], pat, base, cm, allow_small_or_imprecise_dtypes=True), [out], list(after))
        else:
            op("g", lambda: g.iota(out[0], pat, base, cm), [out], [])

    def dma_now(q, out, a, after):
        need(q, a[1], out[1] + after)
        sem = "d%d" % ndma[0]
        ndma[0] += 1
        done(q, queue[q].dma_start(out[0], a[0]), a[1], out[1], sem, 16)

    def dma(q, out, a, after=()):
        size = max(out[2] * (4 if out[1] and wide(out) else 2), a[2] * (4 if a[1] and wide(a) else 2))
        moved[len(calls)] = COST["byte"] * size
        also[len(calls)] = list(after)
        soon[len(calls)] = SOON.get(out[1][0][0], 0.0) if out[1] else 0.0
        calls.append((q, lambda: dma_now(q, out, a, list(after)), list(a[1]), list(out[1]), COST["dma"], COST["load"]))

    def hbm(ap):
        return (ap, [], 0)

    def send_now(pairs, sem):
        need("g", [r for x in pairs for r in x[2][1]], [])
        tr = []
        for j, (s, q, a, o) in enumerate(pairs):
            eng = topo.engines(core, T.cores[q])
            n = len(eng) // len(pairs)
            rid, pid, se = topo.addr(T.cores[q])
            count["lsem"] = count.get("lsem", 0) + n
            if len(pairs) == 1:
                g.remote_dma(o, a[0], T.sem["%s%d" % (sem, s)], T.sem.lsem, pid, rid, topo.mask(core, T.cores[q]))
                return
            tr.append(RemoteDMATransfer(dst_ids=[DstId(rid=rid, pnc=pid)], dma_engine_mask=sum(1 << e for e in eng[n * j:n * j + n]),
                                        remote_sem=T.sem["%s%d" % (sem, s)], src=a[0], dst=o))
        g.remote_dma_fused(tr, local_sem=T.sem.lsem)

    def send(pairs, sem):
        size = len(pairs) * pairs[0][2][2] * (4 if wide(pairs[0][2]) else 2)
        moved[len(calls)] = 2 * COST["byte"] * size
        soon[len(calls)] = SOON.get(sem, 0.0)
        calls.append(("g", lambda: send_now(pairs, sem), regs([x[2] for x in pairs]), regs([LAND[sem](x[0]) for x in pairs]) + [LINK] * (sem in ("lr", "la")),
                      COST["call"] + (COST["first"] if sem == "rn" else 0), COST["far"]))

    def hops(d):
        a, b = topo.chip(T.cores[0]), topo.chip(T.cores[d])
        return 2 if topo.mates(a, b) else 1 if topo.same_plane(a, b) else 0

    DIST = sorted(range(1, N), key=lambda d: (hops(d), (d // 4 + hops(d) + 1) % 2))
    DIST.insert(S0, 0)
    owner = [me ^ d for d in DIST]
    asker = owner
    FAR = [s for s in range(N) if s != S0]

    def arrives(sem, s, src, view, together):
        n = len(topo.engines(T.cores[src], core)) // together
        name = "%s%d" % (sem, s)
        count[name] = n
        seen_by[(name, n)] = {name: n}
        for (k, lo, hi) in view[1]:
            log.setdefault(k, []).append((lo, hi, True, (name, n), "remote"))

    LAND = {"rn": lambda s: V3("rn", s, s + 1, 0, 2), "rl": lambda s: V2("rl", 48 * s, 48 * s + 48), "rq": lambda s: V3("rq", s, s + 1, 0, 48),
            "lr": lambda s: V2("lr", LC * s, LC * s + LC), "la": lambda s: V2("land", SW * s, SW * s + CAPQ)}
    for s in FAR:
        for m in LAND:
            arrives(m, s, asker[s], LAND[m](s), N - 1 if m == "rn" else [len(gr) for gr in GRP if s in gr][0])

    dma("y", V2("sdI"), hbm(T.sd[:]))
    fill(V2("rkI"), 0)
    dma("s", V2("rkI", p=slice(0, 128, 16)), hbm(T.rk[:]))
    dma("y", V2("thrI"), hbm(T.thr[:]), V2("sdI")[1])
    dma("y", V2("aliI"), hbm(T.ali[:]), V2("sdI")[1])
    dma("y", V2("seenS"), hbm(T.seen[:]), V2("rkI")[1])
    dma("y", V2("vecS", 0, 1024), hbm(T.vec[:, 0:1024]), V2("seenS")[1])

    fill(V2("oneb"), 1.0)
    fill(V2("rst"), 1.0)
    iota(V2("pI"), [[0, 1]], 0, 1)
    iota(V2("iotaK"), [[5 * 1597 - 8192, 64]], 0, 0)
    iota(V2("gC"), [[1, 8], [0, 16]], 0, 0, True)
    ts(V2("pg"), V2("pI"), 4, None, A.arith_shift_right)
    cp(V2("pgF"), V2("pg"))
    for nm, c in (("G1", 1.0), ("G64", 64.0), ("BDf", 1.0), ("BD", 1.0)):
        ts(V2(nm), V2("gC"), V2("pgF"), c, A.is_equal, A.mult)
    act(V2("Gc"), V2("BD"), scale=-8192.0)
    iota(V2("uC", 0, 256 // PARTS), [[0, 16 // PARTS], [1, 16]], 0, 0, True)
    iota(V2("w1c"), [[1, 8]], 0, 0, True)
    iota(V2("iotaC"), [[1597, 4], [7985, 4], [0, 16]], 1597 + 2048, 0, True)
    aff(V2("Id"), V2("oneb", 0, 128), [[-1, 128]], A.is_equal, 0, 1)
    aff(V2("Tri"), V2("BD"), [[1, 128]], A.is_gt, 0, -1)
    for z in range(3):
        iota(V2("Vwin", 512 * z, 512 * z + 512), [[0, 512]], 0, 0, True)
    fill(V2("rst", 0, 512, 64), 0.0)
    fill(V2("Zs"), 0.0)
    ts(V2("pm"), V2("pI"), 15, None, A.bitwise_and)
    fill(V2("Zs", 15, 144, 16), 1.0)
    cp(V2("pmF"), V2("pm"))
    ts(V2("cxF"), V2("pm"), 4.0 * 7985.0, None, A.mult)

    for z in range(2):
        act(V2("VxS", 512 * z, 512 * z + 512), V2("rst"), scale=0.0)
    ts(V2("loI"), V2("sdI"), 4095, None, A.bitwise_and)
    ts(V2("hiI"), V2("sdI"), 12, None, A.arith_shift_right)

    own = V2("b3", 0, 64)
    IdM = V2("Id")
    f2 = V2("b5", 0, 64)
    cnt = V2("Pc", 63, 512, 64)

    def owners():
        cp(V2("sdF"), V2("sdI"))
        ts(V2("hpF"), V2("hiI"), 64.0, -262144.0, A.mult, A.add)
        ts(V2("Lr"), V2("iotaK"), V2("sdF"), None, A.add)
        cp(V2("rkF"), V2("rkI"))
        ts(V2("Lq"), V2("Lr"), 4095, None, A.bitwise_and)
        mm(V2("b4", 0, 16), V2("BDf"), V2("rkF"), True, True)
        tt(V2("b6", 0, 64), V2("Lq"), V2("Lq"), A.mult)
        act(V2("w4c"), V2("w1c"), scale=4096.0)
        ts(V2("t1"), V2("b6", 0, 64), V2("hpF"), None, A.add)
        ts(V2("Lp"), V2("Lq"), 64.0, -262144.0, A.mult, A.add)
        ts(V2("Bq"), V2("t1"), 6, 4095, A.arith_shift_right, A.bitwise_and)
        tt(V2("tA"), V2("w4c"), V2("b4", 0, 8), A.add)
        tt(V2("b6", 64, 128), V2("Bq"), V2("Bq"), A.mult)
        tt(V2("dA"), V2("b4", 8, 16), V2("w1c"), A.subtract)
        tt(V2("t2"), V2("Lp"), V2("b6", 64, 128), A.add)
        ts(V2("dB"), V2("dA"), -1.0, 1.0, A.mult, A.add)
        ts(V2("w12"), V2("t2"), 3, 28672, A.arith_shift_right, A.bitwise_and)
        act(V2("s256"), V2("w1c"), scale=float(SW))
        tt(V2("Zk"), V2("w12"), V2("Bq"), A.add)
        cp(V2("I1"), V2("Id"))
        op("s", lambda: g.scalar.activation(T.dH[:, 0:7], T.dB[:, 0:7], F.Copy, scale=0.5, accum_out=T.dH[:, 7:8]), [V2("dH")], [V2("dB")])
        dg = [V2("W1", 1024 + 128 * w, 1152 + 128 * w) for w in range(8)]
        for w in range(8):
            act(dg[w], IdM, scale=V2("dH", w, w + 1))
        mm(own, dg[7], V2("oneb", 0, 64), True, False)
        fill(V2("W1", 960, 1024), 0.0)
        for w in range(8):
            ts(V2("W1", 128 * w, 128 * w + 64), V2("Zk"), V2("tA", w, w + 1), V2("dA", w, w + 1), A.is_ge, A.mult)
            mm(own, IdM, V2("W1", 128 * w, 128 * w + 64), False, w == 7)
            if w < 7:
                act(V2("W1", 128 * w + 64, 128 * w + 128), V2("Zk"), F.Sign, bias=0.5 - 4096.0 * (w + 1))
                mm(own, dg[w], V2("W1", 128 * w + 64, 128 * w + 128), False, False)
        for s in range(N):
            ts(V2("b2", 64 * s, 64 * s + 64), own, float(owner[s]), None, A.is_equal)
        for a in range(0, 512, SC):
            scan(V2("Pc", a, a + SC), V2("rst", a, a + SC), V2("b2", a, a + SC), A.mult, A.add)
        act(V2("ownb"), own)
        mm(V2("b4", 24, 32), IdM, V2("s256"), True, False)
        mm(V2("b4", 24, 32), V2("Tri"), cnt, False, True)
        mm(V2("b1", 256, 264), V2("Tri"), cnt, True, True)
        for a in range(0, 512, SC):
            tt(V2("Dc", a, a + SC), V2("Pc", a, a + SC), V2("b2", a, a + SC), A.mult)
        for s in range(N):
            mm(f2, IdM, V2("Dc", 64 * s, 64 * s + 64), s == 0, False)
        for s in range(N):
            ts(V2("Of", 64 * s, 64 * s + 64), V2("ownb"), float(owner[s]), V2("b4", 24 + s, 25 + s), A.is_equal, A.mult)
            mm(f2, V2("I1"), V2("Of", 64 * s, 64 * s + 64), False, s == N - 1)
        fill(V3("rnS", 0, N, 0, 2), 0.0)
        act((T.rnS[:, :, 0], V3("rnS", 0, N, 0, 1)[1], N), V2("b1", 256, 264))
        ts(V2("fh"), f2, 0.0625, -8.5 / 16, A.mult, A.add)
        ts(V2("fa"), f2, 96.0, -96.0, A.mult, A.add)
        ts(V2("b6", 0, 64), V2("fh"), -1535.0, None, A.mult)
        tt(V2("F2u"), V2("fa"), V2("b6", 0, 64), A.add)

    def cands():
        ts(V2("loC"), V2("loI"), -2048.0, None, A.add)
        ts(V2("hiC"), V2("hiI"), -2048.0, None, A.add)
        w = 256 // PARTS
        ts(V2("Rlo", 0, w), V2("uC", 0, w), V2("pmF"), V2("loC"), A.is_equal, A.mult)
        mm(V2("b0", 0, w), V2("G1"), V2("Rlo", 0, w), True, True)
        ts(V2("Rhi", 0, w), V2("uC", 0, w), V2("pmF"), V2("hiC"), A.is_equal, A.mult)
        mm(V2("b7", 0, w), V2("Gc"), V2("oneb", 0, w), True, False)
        mm(V2("b7", 0, w), V2("G64"), V2("Rhi", 0, w), False, True)
        act(V2("nC"), V2("iotaC"), F.Identity, bias=V2("cxF"))
        for a in range(0, 256, w):
            def H(nm, o=0):
                return V2(nm, o + a, o + a + w)
            tt(H("hx"), H("nC"), V2("b0", 0, w), A.add)
            ts(H("hL"), H("hx"), 4095, None, A.bitwise_and)
            cp(H("Lf"), H("hL"))
            act(H("hq"), H("Lf"), F.Square)
            act(H("b1"), H("Lf"), F.Identity, scale=64.0, bias=-262144.0)
            tt(H("ht"), H("hq"), V2("b7", 0, w), A.add)
            ts(H("hB"), H("ht"), 6, 4095, A.arith_shift_right, A.bitwise_and)
            cp(H("Bf"), H("hB"))
            act(H("hb"), H("Bf"), F.Square)
            act(H("b7", 256), H("Bf"), scale=4096.0)
            tt(H("hu"), H("hb"), H("b1"), A.add)
            ts(H("he"), H("hu"), 7, 2047, A.arith_shift_right, A.bitwise_and)
            tt(H("hv"), H("he"), H("b7", 256), A.add)
            for v in range(a // 64, (a + w) // 64):
                dma("y", row("VxS", v), V2("hv", 64 * v, 64 * v + 64), [("VxS", 0, 1024)])

    def scatter():
        send([(s, owner[s], V3("rnS", s, s + 1, 0, 2), T.rn[:, s, :]) for s in FAR], "rn")
        calls[-1][3].append(("turn", 0, 1))
        iota(V2("jc"), [[16, LC], [0, 3], [1, 16]], 0, 0, True)
        calls[-1][3].append(("turn", 0, 1))
        iota(V2("p4"), [[1, 128]], 0, 0, True)
        aff(V2("Za"), V2("Zs"), [[-16, 9], [0, 16]], A.is_ge, 0, 1)
        calls[-1][3].append(("turn", 0, 1))
        aff(V2("Zt"), V2("Za"), [[16, 9], [0, 16]], A.is_ge, 2, -1)
        aff(V2("Zs"), V2("Za"), [[16, 9], [0, 16]], A.is_ge, 15, -1)
        fill(E("sI", 0, N, 0, 1), 0)
        aff(V2("Zi"), V2("Zs"), [[-16, 9], [0, 16]], A.is_ge, -3, 1)
        aff(V2("Zi"), V2("Zi"), [[16, 9], [0, 16]], A.is_ge, 4, -1)
        dma("y", V2("vecS", 1024, 2048), (T.vec[:, 1024:2048], rows("VxS")[1], 0))
        cp(IX(V2("Vwin"), V2("F2u")), rows("VxS"))
        for v in range(4):
            dma(FQ[v % 2], V2("fv", 96 * v, 96 * v + 96), (T.Vwin[v:128:16, :], V2("Vwin")[1], 96))
            calls[-1][3].append(("fold", 0, 1))

    def lists():
        for i in range(4):
            ts(V2("b6", 96 * i, 96 * i + 96), V2("fv", 96 * i, 96 * i + 96), 1.5 * 2 ** 35, 1.5 * 2 ** 35, A.add, A.subtract)
        for i in range(4):
            x = slice(0, LC) if i == 3 else slice(LC + 2 - i, 48, 3)
            le, msg = ((T[nm][:, :, x], [(nm, 48 * s + x.start, 48 * s + x.start + 1) for s in range(N)], N * LC) for nm in ("le", "msg"))
            y, r = V2("fv", 96 * i, 96 * i + 96), V2("b6", 96 * i, 96 * i + 96)
            tt(le, y, r, A.subtract)
            calls[-1][2].extend(V2("b6", 96 * LT, 96 * LT + 96)[1])
            act(msg, y, F.Identity, bias=2048.0)
            calls[-1][2].extend(V2("seenD", 0, MS)[1])
        act(V3("rq", S0, S0 + 1, 0, 48), V3("msg", S0, S0 + 1, 0, 48))
        for m, k in SENDS:
            send([(s, owner[s], V3("le" if m == "rl" else "msg", s, s + 1, 0, 48), T.rl[:, 48 * s:48 * s + 48] if m == "rl" else T.rq[:, s, :]) for s in GRP[k]], m)
            calls[-1][3].append(("turn", 0, 1))

    def table():
        for j in (3, 4, 0, 1, 2):
            dma("y", row("W1", j), V2("p%d" % j), V2("W1")[1])
            calls[-1][3].extend([("fold", 0, 1)] * (j < 3))

    def pieces():
        ts(V2("c0", 2, 3), V2("pm"), 128.0, None, A.mult)
        act(V2("p3"), V2("oneb", 0, 128), scale=V2("c0", 2, 3))
        t0, t1, t2 = (V2(PB, 128 * z, 128 * z + 128) for z in (1, 2, 3))
        ts(t0, V2("thrI"), 4096.0, None, A.mult)
        tt(t1, V2("aliI"), t0, A.add)
        cp(V2("p0"), t1)
        calls[-1][2].extend(V2("Vwin")[1])
        tt(t2, t1, V2("p0"), A.subtract)
        cp(V2("p1"), t2)
        tt(V2("p2"), t2, V2("p1"), A.subtract)
    tab = rows("W1")

    def tables():
        def M(k):
            return V2("Md", 128 * k, 128 * k + 128)
        act(M(0), V2("BD"), scale=-1.0)
        aff(M(0), M(0), [[1, 128]], A.is_equal, -1, -1)
        op("g", lambda: g.affine_select(M(0)[0], M(0)[0], [[-1, 128]], A.not_equal, 1.0, 0, 1), [M(0)], [M(0)])
        for k, a, c in ((1, M(0), 16.0), (2, M(0), 1.0 / 16), (3, IdM, -16.0)):
            act(M(k), a, scale=c)
            due[len(calls) - 1] = 26.0
        ts(V2("c0", 1, 2), V2("pmF"), 0.0, -17.0 * 192, A.is_equal, A.mult)
        for z in range(2):
            dma("y", V2("aliJ", 64 * z, 64 * z + 64), hbm(T.ali[:, 1024 * z:1024 * z + 1024]), V2("rkI")[1])
        cp(V2("aliU"), V2("aliJ"))
        for o in range(0, 2048, HW):
            if o < HV:
                ts(V2("hS", o, o + HW), V2("seenS", o, o + HW), 3072 - 7.5, None, A.add)
            else:
                act(V2("hS", o, o + HW), V2("seenS", o, o + HW), F.Identity, bias=3072 - 7.5)
                calls[-1][2].extend(V2("hb")[1])
        for z in range(4):
            act(V2("sA", 512 * z, 512 * z + 512), IX(V2("seenS"), V2("aliU", 32 * z, 32 * z + 32)))
            calls[-1][2].extend(V3("rnS", 0, N, 0, 1)[1] if z >= RZ else V2("hb")[1])
            act(V2("hA", 512 * z, 512 * z + 512), V2("sA", 512 * z, 512 * z + 512), F.Identity, bias=3072 - 7.5)
        for n, (h, k, nm, ka, na) in enumerate(((1, 2, "hS", 0, "hA"), (0, 0, "seenS", 1, "sA"))):
            for z in range(4):
                bank, o = HB[4 * n + z], 1024 * (z // 2)
                mm(V2(bank), M(k), V2(nm, 512 * z, 512 * z + 512), True, False)
                calls[-1][2].extend(V2("fh")[1])
                run([(V2(bank, 64 * p, 64 * p + 64), M(ka), V2(na, o + 8 * (z % 2) + p, o + 1024, 16), False, h == 1 and p == 7) for p in range(8)])
                if not h:
                    mm(V2(bank), M(3), V2("seenD", 2048 + 512 * z, 2560 + 512 * z), False, True)
                o = V2("seenD", 2048 * h + 512 * z, 2048 * h + 512 * z + 512)
                if 4 * n + z in EV:
                    cp(o, V2(bank))
                    calls[-1][2].extend(V2("Vwin")[1])
                else:
                    act(o, V2(bank), F.Identity, bias=V2("c0", 1, 2) if h else 0.0)
                due[len(calls) - 1] = DUT[n] - 0.1 * z

    def masks():
        for s in range(N):
            ts(V2("mk", 576 * s, 576 * s + 576), V2("jc"), V3("rnS" if s == S0 else "rn", s, s + 1, 0, 1), float(2 ** (16 - asker[s] % 4)), A.is_ge, A.mult)
            calls[-1][2].extend(V2("Vwin")[1] if s in MK else V3("le", 0, N, 0, 48)[1])

    def ylist():
        ts(V2("yo"), f2, -1.0, None, A.add)
        calls[-1][2].extend(V2("Vwin")[1])
        act(V2("own2k"), V2("ownb"), scale=2048.0)

    def look(c):
        a, b = CH[c]
        for s in range(a, b):
            for f, u, v in [(cp, u, min(u + GW, GV[s])) for u in range(0, GV.get(s, 0), GW)] + [(act, GV.get(s, 0), 48)]:
                if u < v:
                    lst = (T.le[:, s, u:v], V3("le", s, s + 1, 0, 48)[1], v - u) if s == S0 else V2("rl", 48 * s + u, 48 * s + v)
                    f(V2("GT", 768 * s + 16 * u, 768 * s + 16 * v), IX(tab, lst))

    def arrive(c):
        a, b = CH[c]
        back(V2(TB[c], 0, 48 * (b - a)), "Zt", "GT", 768 * a, 768 * b)

    def filt(c):
        a, b = CH[c]
        tt(V3("mn", a, b, 0, 48), V3("rq", a, b, 0, 48), V2(TB[c], 0, 48 * (b - a)), A.min)
        tt(V3("fl", a, b, 0, 48), V3("rq", a, b, 0, 48), V2(TB[c], 0, 48 * (b - a)), A.is_lt)
        ts(E("cI", a, b, 0, 1), V3("mn", a, b, 0, LC), 2047, None, A.bitwise_and)
        ts(E("cI", a, b, 1, 4), V3("mn", a, b, LC, 48), 2047, None, A.bitwise_and)
        ts(V2("fac", 36 * a, 36 * b), V3("fl", a, b, LC, 48), 15.0, 1.0, A.mult, A.add)
        w = MGW[c]
        for s in range(a, b):
            for u in range(0, 36, w):
                o, h = 36 * s + u, 2048 * (asker[s] // 4)
                lst = (T.le[:, s, LC + u:LC + u + w], V3("le", s, s + 1, 0, 48)[1], w) if s == S0 else V2("rl", 48 * s + LC + u, 48 * s + LC + u + w)
                tt(V2("MG", 16 * o, 16 * (o + w)), IX(V2("seenD", h, h + 2048), lst), V2("mk", 16 * o, 16 * (o + w)), A.mult)
                due[len(calls) - 1] = DUE[c]
                long.add(len(calls) - 1)

    def pick(c):
        a, b = PG[c]
        w, x = (48 * a, 48 * b), (LC * a, LC * b)
        back(V2(FB[c], 0, 36 * (b - a)), "Zs", "MG", 576 * a, 576 * b)
        tt(E("sI", a, b, 1, 4), V2("fac", 36 * a, 36 * b), V2(FB[c], 0, 36 * (b - a)), A.mult)
        ts(V2("sb", *w), E("sI", a, b, 0, 4), 2 ** 20, None, A.bitwise_and)
        tt(V2("kb", *w), E("cI", a, b, 0, 4), V2("sb", *w), A.subtract)
        scan(V2("kc", *w), V2("sb", *w), V2("kb", *w), A.min, A.max)
        cp(V2("lx", *x), V2("kc", 48 * a + 3, 48 * b, 4))
        due[len(calls) - 1] = DUP[c]
        far = [s for s in range(a, b) if s != S0]
        if far:
            act(V2("rs", CAPQ * far[0], CAPQ * far[-1] + CAPQ), IX(V2("vecS"), V2("lx", LC * far[0], LC * far[-1] + LC)))
        if a <= S0 < b:
            act(V2("land", SW * S0, SW * S0 + CAPQ), IX(V2("vecS"), V2("lx", LC * S0, LC * S0 + LC)))

    def answers():
        for m, k in BACK:
            if m == "lr":
                send([(s, asker[s], V2("lx", LC * s, LC * s + LC), T.lr[:, LC * s:LC * s + LC]) for s in GRP[k]], m)
            else:
                send([(s, asker[s], V2("rs", CAPQ * s, CAPQ * s + CAPQ), T.land[:, SW * s:SW * s + CAPQ]) for s in GRP[k]], m)

    def items(c):
        for s in range(*CH[c]):
            (cp if s in IV else act)(V2("IDx", SW * s, SW * s + CAPQ), IX(tab, V2("lx" if s == S0 else "lr", LC * s, LC * s + LC)))
            if s in IL:
                held.append(calls[-1])

    for f in (owners, cands, scatter, pieces, ylist, tables, lists, masks):
        f()
    table()
    for c in range(len(CH)):
        for f in (look, arrive, filt):
            f(c)
    for c in range(len(PG)):
        pick(c)
    answers()
    held = []
    for c in range(len(CH)):
        items(c)
    for x in held:
        x[2].extend(V2("rs" if x[0] == "s" else "lx")[1])

    for h in range(2):
        (cp, act)[h](V2("IDg", 512 * h, 512 * h + 512), IX(V2("IDx"), V2("yo", 32 * h, 32 * h + 32)))
    back(V2("b4", 64, 128), "Zi", "IDg", 0, 1024)
    tt(V2("chS"), V2("own2k"), V2("b4", 64, 128), A.add)
    dma("y", hbm(T.chosen[:]), V2("chS"))
    w = 1024 // YP
    for h in range(YP):
        (cp, act)[h % 2](V2("yS", w * h, w * h + w), IX(V2("land"), V2("yo", w * h // 16, w * (h + 1) // 16)))
        dma("ys"[h % 2], hbm(T.y[:, w * h:w * h + w]), V2("yS", w * h, w * h + w))
    issue()

    for s, n in count.items():
        if clock["g"].get(s, 0) < n:
            g.wait_ge(T.sem[s], n)
